import numpy as np
import ml_dtypes


def mxq(x, axis, fmt="e4m3"):
    dtype, down = {"e4m3": (ml_dtypes.float8_e4m3fn, 7), "e5m2": (ml_dtypes.float8_e5m2, 14)}[fmt]
    v = np.moveaxis(np.asarray(x, np.float32).astype(ml_dtypes.bfloat16).astype(np.float64), axis, -1)
    blocks = v.reshape(v.shape[:-1] + (-1, 32))
    amax = np.abs(blocks).max(-1, keepdims=True)
    byte = np.maximum(np.where(amax > 0, np.frexp(amax)[1] - 1 + 127, 0) - down, 1)
    scale = np.exp2(byte - 127.0)
    codes = (blocks / scale).astype(np.float32).astype(dtype).astype(np.float64)
    return np.moveaxis((codes * scale).reshape(v.shape), -1, axis)


WIDE = False


def mx_kscale(k):
    if not WIDE:
        return np.ones(k)
    levels = np.array([10, -10, 5, -5, 0])
    if k % 512:
        return np.exp2(np.random.permutation(np.resize(levels, k // 32))).repeat(32)
    a = np.empty((k // 512, 16))
    for p in range(k // 512):
        a[p, :8] = np.random.permutation(np.resize(levels, 8))
        for g in range(8):
            far = levels[np.abs(levels - a[p, g]) >= 10]
            a[p, g + 8] = far[np.random.randint(len(far))]
    return np.exp2(a.ravel()).repeat(32)


def f64(x):
    return np.asarray(x).astype(np.float64)


def striped(idx):
    return np.tile(idx.reshape(-1, 16).T, (8, 1)).astype(np.uint16)


def unstriped(offs):
    return offs[:16].T.reshape(-1).astype(np.int64)


def gelu(v):
    return 0.5 * v * (1.0 + np.tanh(np.sqrt(2.0 / np.pi) * (v + 0.044715 * v**3)))


K, T, E, C, H, N = 512, 1024, 4, 256, 1024, 256


def by_expert(wq, xq):
    return np.concatenate([wq[e].T @ xq[:, e * C:(e + 1) * C] for e in range(E)], axis=1)


def setup_inputs():
    n = np.random.standard_normal
    s = mx_kscale(K)[:, None]
    u = mx_kscale(H)
    return {
        "xT": (n((K, T)) * s).astype(np.float32),
        "w1": (n((E, K, H)) / np.sqrt(K) / s[None]).astype(np.float32),
        "w3": (n((E, K, H)) / np.sqrt(K) / s[None] * u[None, None, :]).astype(np.float32),
        "w2": (n((E, H, N)) / np.sqrt(H) / u[None, :, None]).astype(np.float32),
        "gate": np.tile(np.random.uniform(0.2, 1.0, E * C), (N, 1)).astype(np.float32),
        "offs": striped(np.random.permutation(T)[:E * C]),
    }


def reference(xT, w1, w3, w2, gate, offs):
    idx = unstriped(offs)
    xq = mxq(f64(xT)[:, idx], 0, "e4m3")
    h = gelu(by_expert(mxq(f64(w1), 1, "e4m3"), xq))
    h = h * by_expert(mxq(f64(w3), 1, "e4m3"), xq)
    y = by_expert(mxq(f64(w2), 1, "e4m3"), mxq(h, 0, "e4m3"))
    out = np.zeros((N, T))
    out[:, idx] = f64(gate) * y
    return out

@@ -1,0 +1,275 @@
+from contextlib import ExitStack
+
+import concourse.mybir as mybir
+
+K, T, E, C, H, N = 512, 1024, 4, 256, 1024, 256
+FLOPS = 2 * E * C * (2 * K * H + H * N)
+
+F32 = mybir.dt.float32
+BF16 = mybir.dt.bfloat16
+U32 = mybir.dt.uint32
+U16 = mybir.dt.uint16
+U8 = mybir.dt.uint8
+FP8X4 = mybir.dt.float8_e4m3fn_x4
+GELU = mybir.ActivationFunctionType.Gelu_apprx_tanh
+MULT = mybir.AluOpType.mult
+
+P = 128
+HC = 512
+HALF = 128
+GROUP = 512
+STAGES = 2 * E
+AHEAD = 4
+VECTOR_T = (0, 0, 2, 2, 2, 2, 2, 2)
+
+
+def tile_routed_moe_kernel(tc, xT, w1, w3, w2, gate, offs, out):
+    nc = tc.nc
+    with ExitStack() as ctx:
+        lists = ctx.enter_context(tc.tile_pool(name="lists", bufs=1))
+        keep = ctx.enter_context(tc.tile_pool(name="keep", bufs=1))
+        rawc = ctx.enter_context(tc.tile_pool(name="rawc", bufs=2 * AHEAD))
+        raw2 = ctx.enter_context(tc.tile_pool(name="raw2", bufs=3))
+        stage13 = ctx.enter_context(tc.tile_pool(name="stage13", bufs=4))
+        stage2 = ctx.enter_context(tc.tile_pool(name="stage2", bufs=2))
+        wq = ctx.enter_context(tc.tile_pool(name="wq", bufs=3))
+        hid = ctx.enter_context(tc.tile_pool(name="hid", bufs=2))
+        gel = ctx.enter_context(tc.tile_pool(name="gel", bufs=4))
+        psum_ab = ctx.enter_context(tc.psum_pool(name="psum_ab", bufs=3))
+        psum_y = ctx.enter_context(tc.psum_pool(name="psum_y", bufs=2))
+
+        offsets = lists.tile([P, T // 16], U16, name="offsets")
+        nc.sync.dma_start(offsets[:], offs)
+
+        warm = keep.tile([P, 1], F32, name="warm")
+        warmed = keep.tile([P, 1], F32, name="warmed")
+        nc.gpsimd.memset(warm[:], 0.0)
+        nc.scalar.activation(out=warmed[:], in_=warm[:], func=GELU)
+
+        x_rows = xT.rearrange("(p t) n -> p t n", t=4)
+        planes = [keep.tile([P, T], F32, name="plane%d" % t) for t in range(4)]
+        gates = [keep.tile([P, E * C], F32, name="gate%d" % nb) for nb in range(2)]
+        windows = [keep.tile([P, T], F32, name="window%d" % nb) for nb in range(2)]
+        gathered = [keep.tile([P, 4, GROUP], F32, name="g4_%d" % gi) for gi in range(E * C // GROUP)]
+        sources = {"a": w1, "b": w3}
+        raw, grouped, codes, scales = {}, {}, {}, {}
+        raw_w2, grouped_w2, q_w2 = {}, {}, {}
+        xg, x_codes, x_scales = {}, {}, {}
+        banks, gelus, hidden, sums, ys = {}, {}, {}, {}, {}
+
+        def load_plane(t):
+            nc.sync.dma_start(out=planes[t][:], in_=x_rows[:, t, :])
+
+        def load_gates():
+            for nb in range(2):
+                nc.sync.dma_start(out=gates[nb][:], in_=gate[P * nb : P * (nb + 1), :])
+
+        def load_chunk(m, u):
+            raw[m, u] = rawc.tile([P, 4, HC], F32, name="rawc")
+            cols = slice(HC * (u % 2), HC * (u % 2 + 1))
+            nc.sync.dma_start(
+                out=raw[m, u][:], in_=sources[m][u // 2, :, :].rearrange("(p j) c -> p j c", j=4)[:, :, cols]
+            )
+
+        def load_w2(e):
+            raw_w2[e] = raw2.tile([P, 2, 4, N], F32, name="raw2")
+            nc.sync.dma_start(out=raw_w2[e][:], in_=w2[e, :, :].rearrange("(g p j) n -> p g j n", g=2, j=4))
+
+        def gather(gi, t):
+            nc.vector.tensor_copy(
+                out=gathered[gi][:, t, :],
+                in_=planes[t][:].indirect(offsets[:, GROUP * gi // 16 : GROUP * (gi + 1) // 16]),
+            )
+
+        def copy_x(e):
+            col0 = e * C % GROUP
+            xg[e] = keep.tile([P, C, 4], BF16, name="xg%d" % e, align_bytes=64)
+            nc.scalar.copy(
+                out=xg[e][:].rearrange("p (c i) t -> p c t i", i=4),
+                in_=gathered[e * C // GROUP][:, :, col0 : col0 + C].rearrange("p t (c i) -> p c t i", i=4),
+            )
+
+        def quantise_x(e):
+            x_codes[e] = keep.tile([P, C], U32, name="xc%d" % e, align_bytes=64)
+            x_scales[e] = keep.tile([P, C], U8, name="xs%d" % e, align_bytes=64)
+            nc.vector.quantize_mx(
+                out=x_codes[e][:].bitcast(FP8X4), scales=x_scales[e][:], in_=xg[e][:].rearrange("p n t -> p (n t)")
+            )
+
+        def views(m, u, t0, t1):
+            dst = grouped[m, u][:, HC * t0 : HC * t1].rearrange("p (t i j) -> p i j t", t=t1 - t0, j=4)
+            src = raw[m, u][:].rearrange("p j (i t) -> p i j t", t=4)[:, :, :, t0:t1]
+            return dst, src
+
+        def copy_chunk_scalar(m, u, vector_t):
+            grouped[m, u] = stage13.tile([P, 4 * HC], BF16, name="grouped13", align_bytes=64)
+            dst, src = views(m, u, 0, 4 - vector_t)
+            nc.scalar.copy(out=dst, in_=src)
+
+        def copy_chunk_vector(m, u, vector_t):
+            if vector_t > 0:
+                dst, src = views(m, u, 4 - vector_t, 4)
+                nc.vector.tensor_copy(out=dst, in_=src)
+
+        def quantise_chunk(m, u):
+            codes[m, u] = wq.tile([P, HC], U32, name="c" + m, align_bytes=64)
+            scales[m, u] = wq.tile([P, HC], U8, name="s" + m, align_bytes=64)
+            nc.vector.quantize_mx(out=codes[m, u][:].bitcast(FP8X4), scales=scales[m, u][:], in_=grouped[m, u][:])
+
+        def copy_w2(e):
+            grouped_w2[e] = stage2.tile([P, 2, N, 4], BF16, name="grouped2", align_bytes=64)
+            for g in range(2):
+                nc.vector.tensor_copy(
+                    out=grouped_w2[e][:, g, :, :].rearrange("p (c i) j -> p c j i", i=4),
+                    in_=raw_w2[e][:, g, :, :].rearrange("p j (c i) -> p c j i", i=4),
+                )
+
+        def quantise_w2(e):
+            c2 = wq.tile([P, 2, N], U32, name="cw2", align_bytes=64)
+            s2 = wq.tile([P, 2, N], U8, name="sw2", align_bytes=64)
+            nc.vector.quantize_mx(
+                out=c2[:].rearrange("p g n -> p (g n)").bitcast(FP8X4),
+                scales=s2[:].rearrange("p g n -> p (g n)"),
+                in_=grouped_w2[e][:].rearrange("p g n j -> p (g n j)"),
+            )
+            q_w2[e] = (c2, s2)
+
+        def first_layer(u):
+            e = u // 2
+            for m in ("a", "b"):
+                for s in range(2):
+                    banks[m, u, s] = psum_ab.tile([P, 4, HALF], F32, name="p" + m)
+                    for t in range(4):
+                        nc.tensor.matmul_mx(
+                            out=banks[m, u, s][:, t, :],
+                            lhsT=codes[m, u][:, P * t : P * (t + 1)].bitcast(FP8X4),
+                            lhsT_scale=scales[m, u][:, P * t : P * (t + 1)],
+                            rhs=x_codes[e][:, HALF * s : HALF * (s + 1)].bitcast(FP8X4),
+                            rhs_scale=x_scales[e][:, HALF * s : HALF * (s + 1)],
+                            start=True,
+                            stop=True,
+                        )
+
+        def hidden_values(u):
+            e, hc = u // 2, u % 2
+            if hc == 0:
+                hidden[e] = hid.tile([P, 2, 2, HALF, 4], BF16, name="hg", align_bytes=64)
+            for s in range(2):
+                gelus[u, s] = gel.tile([P, HALF, 4], F32, name="ga")
+                nc.scalar.activation(out=gelus[u, s][:], in_=banks["a", u, s][:].rearrange("p t n -> p n t"), func=GELU)
+            for s in range(2):
+                nc.vector.tensor_tensor(
+                    out=hidden[e][:, s, hc, :, :],
+                    in0=banks["b", u, s][:].rearrange("p t n -> p n t"),
+                    in1=gelus[u, s][:],
+                    op=MULT,
+                )
+
+        def second_layer(e, lo, hi):
+            parts = hi - lo
+            h_codes = hid.tile([P, parts, 2, HALF], U32, name="hcodes", align_bytes=64)
+            h_scales = hid.tile([P, parts, 2, HALF], U8, name="hscales", align_bytes=64)
+            nc.vector.quantize_mx(
+                out=h_codes[:].rearrange("p s g n -> p (s g n)").bitcast(FP8X4),
+                scales=h_scales[:].rearrange("p s g n -> p (s g n)"),
+                in_=hidden[e][:, lo:hi, :, :, :].rearrange("p s g n t -> p (s g n t)"),
+            )
+            c2, s2 = q_w2[e]
+            sums[e, lo] = psum_y.tile([P, parts, 2, HALF], F32, name="py")
+            for s in range(parts):
+                for nb in range(2):
+                    for g in range(2):
+                        nc.tensor.matmul_mx(
+                            out=sums[e, lo][:, s, nb, :],
+                            lhsT=c2[:, g, P * nb : P * (nb + 1)].bitcast(FP8X4),
+                            lhsT_scale=s2[:, g, P * nb : P * (nb + 1)],
+                            rhs=h_codes[:, s, g, :].bitcast(FP8X4),
+                            rhs_scale=h_scales[:, s, g, :],
+                            start=(g == 0),
+                            stop=(g == 1),
+                        )
+
+        def copy_y(e, lo, hi):
+            ys[e, lo] = hid.tile([P, 2, hi - lo, HALF], F32, name="y")
+            nc.scalar.copy(out=ys[e, lo][:], in_=sums[e, lo][:].rearrange("p s b n -> p b s n"))
+
+        def scatter(e, lo, hi, nb):
+            first, last = C * e + HALF * lo, C * e + HALF * hi
+            nc.vector.tensor_tensor(
+                out=windows[nb][:].indirect(offsets[:, first // 16 : last // 16]),
+                in0=ys[e, lo][:, nb, :, :].rearrange("p s n -> p (s n)"),
+                in1=gates[nb][:, first:last],
+                op=MULT,
+            )
+
+        for c in range(4):
+            load_plane(c)
+            load_chunk("ab"[c % 2], c // 2)
+        load_w2(0)
+        load_chunk("a", 2)
+        load_chunk("b", 2)
+        load_gates()
+        load_w2(1)
+        load_chunk("a", 3)
+        load_chunk("b", 3)
+
+        gather(0, 0)
+        gather(1, 0)
+        for k in range(STAGES):
+            e, hc = k // 2, k % 2
+            copy_chunk_scalar("a", k, 0)
+            if k < 2:
+                gather(0, 2 * k + 1)
+            quantise_chunk("a", k)
+            if k < 2:
+                gather(1, 2 * k + 1)
+            if k == 1:
+                copy_x(0)
+            copy_chunk_scalar("b", k, VECTOR_T[k])
+            if k == 0:
+                gather(0, 2)
+            copy_chunk_vector("b", k, VECTOR_T[k])
+            if k == 1:
+                quantise_x(0)
+            quantise_chunk("b", k)
+            if k == 0:
+                gather(1, 2)
+            if k == 1:
+                first_layer(0)
+            if k >= 1:
+                first_layer(k)
+            if k + AHEAD < STAGES:
+                load_chunk("a", k + AHEAD)
+                load_chunk("b", k + AHEAD)
+                if hc == 0:
+                    load_w2((k + AHEAD) // 2)
+            if k >= 2 and hc == 0:
+                copy_y(e - 1, 0, 2)
+            if hc == 1 and e + 1 < E:
+                copy_x(e + 1)
+            if k == 1:
+                copy_w2(0)
+            if hc == 1:
+                quantise_w2(e)
+            if k >= 2:
+                scatter((k - 2) // 2, 0, 2, hc)
+            if k == 1:
+                hidden_values(0)
+            if k >= 1:
+                hidden_values(k)
+            if hc == 1 and e + 1 < E:
+                second_layer(e, 0, 2)
+            if hc == 0 and k >= 2:
+                copy_w2(e)
+            if hc == 1 and e + 1 < E:
+                quantise_x(e + 1)
+        for s in range(2):
+            second_layer(E - 1, s, s + 1)
+        for s in range(2):
+            copy_y(E - 1, s, s + 1)
+        for s in range(2):
+            for nb in range(2):
+                scatter(E - 1, s, s + 1, nb)
+
+        for nb in range(2):
+            nc.sync.dma_start(out=out[P * nb : P * (nb + 1), :], in_=windows[nb][:])

@@ -101,8 +101,10 @@ def tile_routed_moe_kernel(tc, xT, w1, w3, w2, gate, offs, out):
             src = raw[m, u][:].rearrange("p j (i t) -> p i j t", t=4)[:, :, :, t0:t1]
             return dst, src
 
-        def copy_chunk_scalar(m, u, vector_t):
+        def room_chunk(m, u):
             grouped[m, u] = stage13.tile([P, 4 * HC], BF16, name="grouped13", align_bytes=64)
+
+        def copy_chunk_scalar(m, u, vector_t):
             dst, src = views(m, u, 0, 4 - vector_t)
             nc.scalar.copy(out=dst, in_=src)
 
@@ -116,13 +118,15 @@ def tile_routed_moe_kernel(tc, xT, w1, w3, w2, gate, offs, out):
             scales[m, u] = wq.tile([P, HC], U8, name="s" + m, align_bytes=64)
             nc.vector.quantize_mx(out=codes[m, u][:].bitcast(FP8X4), scales=scales[m, u][:], in_=grouped[m, u][:])
 
-        def copy_w2(e):
+        def copy_w2(e, on_scalar):
             grouped_w2[e] = stage2.tile([P, 2, N, 4], BF16, name="grouped2", align_bytes=64)
             for g in range(2):
-                nc.vector.tensor_copy(
-                    out=grouped_w2[e][:, g, :, :].rearrange("p (c i) j -> p c j i", i=4),
-                    in_=raw_w2[e][:, g, :, :].rearrange("p j (c i) -> p c j i", i=4),
-                )
+                dst = grouped_w2[e][:, g, :, :].rearrange("p (c i) j -> p c j i", i=4)
+                src = raw_w2[e][:, g, :, :].rearrange("p j (c i) -> p c j i", i=4)
+                if on_scalar:
+                    nc.scalar.copy(out=dst, in_=src)
+                else:
+                    nc.vector.tensor_copy(out=dst, in_=src)
 
         def quantise_w2(e):
             c2 = wq.tile([P, 2, N], U32, name="cw2", align_bytes=64)
@@ -217,6 +221,9 @@ def tile_routed_moe_kernel(tc, xT, w1, w3, w2, gate, offs, out):
         gather(1, 0)
         for k in range(STAGES):
             e, hc = k // 2, k % 2
+            room_chunk("b", k)
+            copy_chunk_vector("b", k, VECTOR_T[k])
+            room_chunk("a", k)
             copy_chunk_scalar("a", k, 0)
             if k < 2:
                 gather(0, 2 * k + 1)
@@ -228,7 +235,6 @@ def tile_routed_moe_kernel(tc, xT, w1, w3, w2, gate, offs, out):
             copy_chunk_scalar("b", k, VECTOR_T[k])
             if k == 0:
                 gather(0, 2)
-            copy_chunk_vector("b", k, VECTOR_T[k])
             if k == 1:
                 quantise_x(0)
             quantise_chunk("b", k)
@@ -248,23 +254,27 @@ def tile_routed_moe_kernel(tc, xT, w1, w3, w2, gate, offs, out):
             if hc == 1 and e + 1 < E:
                 copy_x(e + 1)
             if k == 1:
-                copy_w2(0)
+                copy_w2(0, False)
+            if k == STAGES - 1:
+                copy_w2(e, True)
             if hc == 1:
                 quantise_w2(e)
-            if k >= 2:
+            if 2 <= k < STAGES - 2:
                 scatter((k - 2) // 2, 0, 2, hc)
+            if k == STAGES - 1:
+                scatter(E - 2, 0, 2, 0)
             if k == 1:
                 hidden_values(0)
             if k >= 1:
                 hidden_values(k)
             if hc == 1 and e + 1 < E:
-                second_layer(e, 0, 2)
-            if hc == 0 and k >= 2:
-                copy_w2(e)
-            if hc == 1 and e + 1 < E:
                 quantise_x(e + 1)
+                second_layer(e, 0, 2)
+            if hc == 0 and 2 <= k < STAGES - 2:
+                copy_w2(e, False)
         for s in range(2):
             second_layer(E - 1, s, s + 1)
+        scatter(E - 2, 0, 2, 1)
         for s in range(2):
             copy_y(E - 1, s, s + 1)
         for s in range(2):

@@ -13,6 +13,7 @@ U8 = mybir.dt.uint8
 FP8X4 = mybir.dt.float8_e4m3fn_x4
 GELU = mybir.ActivationFunctionType.Gelu_apprx_tanh
 MULT = mybir.AluOpType.mult
+ADD = mybir.AluOpType.add
 
 P = 128
 HC = 512
@@ -101,10 +102,8 @@ def tile_routed_moe_kernel(tc, xT, w1, w3, w2, gate, offs, out):
             src = raw[m, u][:].rearrange("p j (i t) -> p i j t", t=4)[:, :, :, t0:t1]
             return dst, src
 
-        def room_chunk(m, u):
-            grouped[m, u] = stage13.tile([P, 4 * HC], BF16, name="grouped13", align_bytes=64)
-
         def copy_chunk_scalar(m, u, vector_t):
+            grouped[m, u] = stage13.tile([P, 4 * HC], BF16, name="grouped13", align_bytes=64)
             dst, src = views(m, u, 0, 4 - vector_t)
             nc.scalar.copy(out=dst, in_=src)
 
@@ -118,15 +117,17 @@ def tile_routed_moe_kernel(tc, xT, w1, w3, w2, gate, offs, out):
             scales[m, u] = wq.tile([P, HC], U8, name="s" + m, align_bytes=64)
             nc.vector.quantize_mx(out=codes[m, u][:].bitcast(FP8X4), scales=scales[m, u][:], in_=grouped[m, u][:])
 
-        def copy_w2(e, on_scalar):
+        def copy_w2(e):
             grouped_w2[e] = stage2.tile([P, 2, N, 4], BF16, name="grouped2", align_bytes=64)
             for g in range(2):
-                dst = grouped_w2[e][:, g, :, :].rearrange("p (c i) j -> p c j i", i=4)
-                src = raw_w2[e][:, g, :, :].rearrange("p j (c i) -> p c j i", i=4)
-                if on_scalar:
-                    nc.scalar.copy(out=dst, in_=src)
-                else:
-                    nc.vector.tensor_copy(out=dst, in_=src)
+                nc.gpsimd.tensor_scalar(
+                    out=grouped_w2[e][:, g, :, :],
+                    in0=raw_w2[e][:, g, :, :].rearrange("p j n -> p n j"),
+                    scalar1=1.0,
+                    scalar2=0.0,
+                    op0=MULT,
+                    op1=ADD,
+                )
 
         def quantise_w2(e):
             c2 = wq.tile([P, 2, N], U32, name="cw2", align_bytes=64)
@@ -221,9 +222,6 @@ def tile_routed_moe_kernel(tc, xT, w1, w3, w2, gate, offs, out):
         gather(1, 0)
         for k in range(STAGES):
             e, hc = k // 2, k % 2
-            room_chunk("b", k)
-            copy_chunk_vector("b", k, VECTOR_T[k])
-            room_chunk("a", k)
             copy_chunk_scalar("a", k, 0)
             if k < 2:
                 gather(0, 2 * k + 1)
@@ -235,6 +233,7 @@ def tile_routed_moe_kernel(tc, xT, w1, w3, w2, gate, offs, out):
             copy_chunk_scalar("b", k, VECTOR_T[k])
             if k == 0:
                 gather(0, 2)
+            copy_chunk_vector("b", k, VECTOR_T[k])
             if k == 1:
                 quantise_x(0)
             quantise_chunk("b", k)
@@ -254,27 +253,23 @@ def tile_routed_moe_kernel(tc, xT, w1, w3, w2, gate, offs, out):
             if hc == 1 and e + 1 < E:
                 copy_x(e + 1)
             if k == 1:
-                copy_w2(0, False)
-            if k == STAGES - 1:
-                copy_w2(e, True)
+                copy_w2(0)
             if hc == 1:
                 quantise_w2(e)
-            if 2 <= k < STAGES - 2:
+            if k >= 2:
                 scatter((k - 2) // 2, 0, 2, hc)
-            if k == STAGES - 1:
-                scatter(E - 2, 0, 2, 0)
             if k == 1:
                 hidden_values(0)
             if k >= 1:
                 hidden_values(k)
             if hc == 1 and e + 1 < E:
-                quantise_x(e + 1)
                 second_layer(e, 0, 2)
-            if hc == 0 and 2 <= k < STAGES - 2:
-                copy_w2(e, False)
+            if hc == 0 and k >= 2:
+                copy_w2(e)
+            if hc == 1 and e + 1 < E:
+                quantise_x(e + 1)
         for s in range(2):
             second_layer(E - 1, s, s + 1)
-        scatter(E - 2, 0, 2, 1)
         for s in range(2):
             copy_y(E - 1, s, s + 1)
         for s in range(2):

@@ -13,14 +13,13 @@ U8 = mybir.dt.uint8
 FP8X4 = mybir.dt.float8_e4m3fn_x4
 GELU = mybir.ActivationFunctionType.Gelu_apprx_tanh
 MULT = mybir.AluOpType.mult
-ADD = mybir.AluOpType.add
 
 P = 128
 HC = 512
 HALF = 128
 GROUP = 512
 STAGES = 2 * E
-AHEAD = 4
+WHOLE = (1, 2)
 VECTOR_T = (0, 0, 2, 2, 2, 2, 2, 2)
 
 
@@ -29,11 +28,12 @@ def tile_routed_moe_kernel(tc, xT, w1, w3, w2, gate, offs, out):
     with ExitStack() as ctx:
         lists = ctx.enter_context(tc.tile_pool(name="lists", bufs=1))
         keep = ctx.enter_context(tc.tile_pool(name="keep", bufs=1))
-        rawc = ctx.enter_context(tc.tile_pool(name="rawc", bufs=2 * AHEAD))
+        rawc = ctx.enter_context(tc.tile_pool(name="rawc", bufs=4))
+        rawbig = ctx.enter_context(tc.tile_pool(name="rawbig", bufs=3))
         raw2 = ctx.enter_context(tc.tile_pool(name="raw2", bufs=3))
         stage13 = ctx.enter_context(tc.tile_pool(name="stage13", bufs=4))
         stage2 = ctx.enter_context(tc.tile_pool(name="stage2", bufs=2))
-        wq = ctx.enter_context(tc.tile_pool(name="wq", bufs=3))
+        wq = ctx.enter_context(tc.tile_pool(name="wq", bufs=2))
         hid = ctx.enter_context(tc.tile_pool(name="hid", bufs=2))
         gel = ctx.enter_context(tc.tile_pool(name="gel", bufs=4))
         psum_ab = ctx.enter_context(tc.psum_pool(name="psum_ab", bufs=3))
@@ -66,11 +66,18 @@ def tile_routed_moe_kernel(tc, xT, w1, w3, w2, gate, offs, out):
                 nc.sync.dma_start(out=gates[nb][:], in_=gate[P * nb : P * (nb + 1), :])
 
         def load_chunk(m, u):
-            raw[m, u] = rawc.tile([P, 4, HC], F32, name="rawc")
+            chunk = rawc.tile([P, 4, HC], F32, name="rawc")
             cols = slice(HC * (u % 2), HC * (u % 2 + 1))
             nc.sync.dma_start(
-                out=raw[m, u][:], in_=sources[m][u // 2, :, :].rearrange("(p j) c -> p j c", j=4)[:, :, cols]
+                out=chunk[:], in_=sources[m][u // 2, :, :].rearrange("(p j) c -> p j c", j=4)[:, :, cols]
             )
+            raw[m, u] = chunk[:]
+
+        def load_matrix(m, e):
+            whole = rawbig.tile([P, 4, H], F32, name="rawbig")
+            nc.sync.dma_start(out=whole[:], in_=sources[m][e, :, :].rearrange("(p j) c -> p j c", j=4))
+            for hc in range(2):
+                raw[m, 2 * e + hc] = whole[:, :, HC * hc : HC * (hc + 1)]
 
         def load_w2(e):
             raw_w2[e] = raw2.tile([P, 2, 4, N], F32, name="raw2")
@@ -99,7 +106,7 @@ def tile_routed_moe_kernel(tc, xT, w1, w3, w2, gate, offs, out):
 
         def views(m, u, t0, t1):
             dst = grouped[m, u][:, HC * t0 : HC * t1].rearrange("p (t i j) -> p i j t", t=t1 - t0, j=4)
-            src = raw[m, u][:].rearrange("p j (i t) -> p i j t", t=4)[:, :, :, t0:t1]
+            src = raw[m, u].rearrange("p j (i t) -> p i j t", t=4)[:, :, :, t0:t1]
             return dst, src
 
         def copy_chunk_scalar(m, u, vector_t):
@@ -120,13 +127,9 @@ def tile_routed_moe_kernel(tc, xT, w1, w3, w2, gate, offs, out):
         def copy_w2(e):
             grouped_w2[e] = stage2.tile([P, 2, N, 4], BF16, name="grouped2", align_bytes=64)
             for g in range(2):
-                nc.gpsimd.tensor_scalar(
-                    out=grouped_w2[e][:, g, :, :],
-                    in0=raw_w2[e][:, g, :, :].rearrange("p j n -> p n j"),
-                    scalar1=1.0,
-                    scalar2=0.0,
-                    op0=MULT,
-                    op1=ADD,
+                nc.vector.tensor_copy(
+                    out=grouped_w2[e][:, g, :, :].rearrange("p (c i) j -> p c j i", i=4),
+                    in_=raw_w2[e][:, g, :, :].rearrange("p j (c i) -> p c j i", i=4),
                 )
 
         def quantise_w2(e):
@@ -211,12 +214,11 @@ def tile_routed_moe_kernel(tc, xT, w1, w3, w2, gate, offs, out):
             load_plane(c)
             load_chunk("ab"[c % 2], c // 2)
         load_w2(0)
-        load_chunk("a", 2)
-        load_chunk("b", 2)
+        load_matrix("a", 1)
+        load_matrix("b", 1)
         load_gates()
         load_w2(1)
-        load_chunk("a", 3)
-        load_chunk("b", 3)
+        load_matrix("a", 2)
 
         gather(0, 0)
         gather(1, 0)
@@ -243,11 +245,13 @@ def tile_routed_moe_kernel(tc, xT, w1, w3, w2, gate, offs, out):
                 first_layer(0)
             if k >= 1:
                 first_layer(k)
-            if k + AHEAD < STAGES:
-                load_chunk("a", k + AHEAD)
-                load_chunk("b", k + AHEAD)
-                if hc == 0:
-                    load_w2((k + AHEAD) // 2)
+            if k == 3:
+                load_matrix("b", 2)
+                load_w2(2)
+                for u in (6, 7):
+                    load_chunk("a", u)
+                    load_chunk("b", u)
+                load_w2(3)
             if k >= 2 and hc == 0:
                 copy_y(e - 1, 0, 2)
             if hc == 1 and e + 1 < E:

@@ -19,8 +19,8 @@ HC = 512
 HALF = 128
 GROUP = 512
 STAGES = 2 * E
-WHOLE = (1, 2)
-VECTOR_T = (0, 0, 2, 2, 2, 2, 2, 2)
+AHEAD = 4
+VECTOR_T = (0, 0, 0, 0, 0, 0, 0, 0)
 
 
 def tile_routed_moe_kernel(tc, xT, w1, w3, w2, gate, offs, out):
@@ -28,12 +28,11 @@ def tile_routed_moe_kernel(tc, xT, w1, w3, w2, gate, offs, out):
     with ExitStack() as ctx:
         lists = ctx.enter_context(tc.tile_pool(name="lists", bufs=1))
         keep = ctx.enter_context(tc.tile_pool(name="keep", bufs=1))
-        rawc = ctx.enter_context(tc.tile_pool(name="rawc", bufs=4))
-        rawbig = ctx.enter_context(tc.tile_pool(name="rawbig", bufs=3))
+        rawc = ctx.enter_context(tc.tile_pool(name="rawc", bufs=2 * AHEAD))
         raw2 = ctx.enter_context(tc.tile_pool(name="raw2", bufs=3))
         stage13 = ctx.enter_context(tc.tile_pool(name="stage13", bufs=4))
         stage2 = ctx.enter_context(tc.tile_pool(name="stage2", bufs=2))
-        wq = ctx.enter_context(tc.tile_pool(name="wq", bufs=2))
+        wq = ctx.enter_context(tc.tile_pool(name="wq", bufs=3))
         hid = ctx.enter_context(tc.tile_pool(name="hid", bufs=2))
         gel = ctx.enter_context(tc.tile_pool(name="gel", bufs=4))
         psum_ab = ctx.enter_context(tc.psum_pool(name="psum_ab", bufs=3))
@@ -66,18 +65,11 @@ def tile_routed_moe_kernel(tc, xT, w1, w3, w2, gate, offs, out):
                 nc.sync.dma_start(out=gates[nb][:], in_=gate[P * nb : P * (nb + 1), :])
 
         def load_chunk(m, u):
-            chunk = rawc.tile([P, 4, HC], F32, name="rawc")
+            raw[m, u] = rawc.tile([P, 4, HC], F32, name="rawc")
             cols = slice(HC * (u % 2), HC * (u % 2 + 1))
             nc.sync.dma_start(
-                out=chunk[:], in_=sources[m][u // 2, :, :].rearrange("(p j) c -> p j c", j=4)[:, :, cols]
+                out=raw[m, u][:], in_=sources[m][u // 2, :, :].rearrange("(p j) c -> p j c", j=4)[:, :, cols]
             )
-            raw[m, u] = chunk[:]
-
-        def load_matrix(m, e):
-            whole = rawbig.tile([P, 4, H], F32, name="rawbig")
-            nc.sync.dma_start(out=whole[:], in_=sources[m][e, :, :].rearrange("(p j) c -> p j c", j=4))
-            for hc in range(2):
-                raw[m, 2 * e + hc] = whole[:, :, HC * hc : HC * (hc + 1)]
 
         def load_w2(e):
             raw_w2[e] = raw2.tile([P, 2, 4, N], F32, name="raw2")
@@ -106,7 +98,7 @@ def tile_routed_moe_kernel(tc, xT, w1, w3, w2, gate, offs, out):
 
         def views(m, u, t0, t1):
             dst = grouped[m, u][:, HC * t0 : HC * t1].rearrange("p (t i j) -> p i j t", t=t1 - t0, j=4)
-            src = raw[m, u].rearrange("p j (i t) -> p i j t", t=4)[:, :, :, t0:t1]
+            src = raw[m, u][:].rearrange("p j (i t) -> p i j t", t=4)[:, :, :, t0:t1]
             return dst, src
 
         def copy_chunk_scalar(m, u, vector_t):
@@ -214,11 +206,12 @@ def tile_routed_moe_kernel(tc, xT, w1, w3, w2, gate, offs, out):
             load_plane(c)
             load_chunk("ab"[c % 2], c // 2)
         load_w2(0)
-        load_matrix("a", 1)
-        load_matrix("b", 1)
+        load_chunk("a", 2)
+        load_chunk("b", 2)
         load_gates()
+        load_chunk("a", 3)
+        load_chunk("b", 3)
         load_w2(1)
-        load_matrix("a", 2)
 
         gather(0, 0)
         gather(1, 0)
@@ -245,13 +238,11 @@ def tile_routed_moe_kernel(tc, xT, w1, w3, w2, gate, offs, out):
                 first_layer(0)
             if k >= 1:
                 first_layer(k)
-            if k == 3:
-                load_matrix("b", 2)
-                load_w2(2)
-                for u in (6, 7):
-                    load_chunk("a", u)
-                    load_chunk("b", u)
-                load_w2(3)
+            if k + AHEAD < STAGES:
+                load_chunk("a", k + AHEAD)
+                load_chunk("b", k + AHEAD)
+                if hc == 1:
+                    load_w2((k + AHEAD) // 2)
             if k >= 2 and hc == 0:
                 copy_y(e - 1, 0, 2)
             if hc == 1 and e + 1 < E:

@@ -13,6 +13,7 @@ U8 = mybir.dt.uint8
 FP8X4 = mybir.dt.float8_e4m3fn_x4
 GELU = mybir.ActivationFunctionType.Gelu_apprx_tanh
 MULT = mybir.AluOpType.mult
+ADD = mybir.AluOpType.add
 
 P = 128
 HC = 512
@@ -21,6 +22,21 @@ GROUP = 512
 STAGES = 2 * E
 AHEAD = 4
 VECTOR_T = (0, 0, 0, 0, 0, 0, 0, 0)
+MERGE_W2 = True
+W2_ON_S = ()
+X0_SOON = False
+W2_LAST_ON_S = False
+TAIL_NB = False
+CUT = 0
+LOADS3 = True
+ONE_RING = False
+ALIAS_G1 = False
+PLANES_FIRST = False
+G1_AT = 0
+X_ON_V = True
+X_EARLY = False
+GPS_X = False
+MERGE_X1 = False
 
 
 def tile_routed_moe_kernel(tc, xT, w1, w3, w2, gate, offs, out):
@@ -28,7 +44,7 @@ def tile_routed_moe_kernel(tc, xT, w1, w3, w2, gate, offs, out):
     with ExitStack() as ctx:
         lists = ctx.enter_context(tc.tile_pool(name="lists", bufs=1))
         keep = ctx.enter_context(tc.tile_pool(name="keep", bufs=1))
-        rawc = ctx.enter_context(tc.tile_pool(name="rawc", bufs=2 * AHEAD))
+        rawc = ctx.enter_context(tc.tile_pool(name="rawc", bufs=2 * AHEAD + 3 if ONE_RING else 2 * AHEAD))
         raw2 = ctx.enter_context(tc.tile_pool(name="raw2", bufs=3))
         stage13 = ctx.enter_context(tc.tile_pool(name="stage13", bufs=4))
         stage2 = ctx.enter_context(tc.tile_pool(name="stage2", bufs=2))
@@ -48,13 +64,18 @@ def tile_routed_moe_kernel(tc, xT, w1, w3, w2, gate, offs, out):
 
         x_rows = xT.rearrange("(p t) n -> p t n", t=4)
         planes = [keep.tile([P, T], F32, name="plane%d" % t) for t in range(4)]
-        gates = [keep.tile([P, E * C], F32, name="gate%d" % nb) for nb in range(2)]
+        if LOADS3:
+            gates = [keep.tile([P, 2, C], F32, name="gate%d" % e) for e in range(E)]
+        else:
+            gates = [keep.tile([P, E * C], F32, name="gate%d" % nb) for nb in range(2)]
         windows = [keep.tile([P, T], F32, name="window%d" % nb) for nb in range(2)]
-        gathered = [keep.tile([P, 4, GROUP], F32, name="g4_%d" % gi) for gi in range(E * C // GROUP)]
+        gathered = [keep.tile([P, 4, GROUP], F32, name="g4_%d" % gi) for gi in range(1 if ALIAS_G1 else E * C // GROUP)]
+        alias = ctx.enter_context(tc.tile_pool(name="alias", bufs=1))
+        pairs = {}
         sources = {"a": w1, "b": w3}
         raw, grouped, codes, scales = {}, {}, {}, {}
         raw_w2, grouped_w2, q_w2 = {}, {}, {}
-        xg, x_codes, x_scales = {}, {}, {}
+        xg, x_codes, x_scales, x_col0 = {}, {}, {}, {}
         banks, gelus, hidden, sums, ys = {}, {}, {}, {}, {}
 
         def load_plane(t):
@@ -64,6 +85,14 @@ def tile_routed_moe_kernel(tc, xT, w1, w3, w2, gate, offs, out):
             for nb in range(2):
                 nc.sync.dma_start(out=gates[nb][:], in_=gate[P * nb : P * (nb + 1), :])
 
+        def load_gate(e):
+            nc.sync.dma_start(out=gates[e][:], in_=gate.rearrange("(b p) n -> p b n", b=2)[:, :, C * e : C * (e + 1)])
+
+        def gate_of(e, nb, lo, hi):
+            if LOADS3:
+                return gates[e][:, nb, HALF * lo : HALF * hi]
+            return gates[nb][:, C * e + HALF * lo : C * e + HALF * hi]
+
         def load_chunk(m, u):
             raw[m, u] = rawc.tile([P, 4, HC], F32, name="rawc")
             cols = slice(HC * (u % 2), HC * (u % 2 + 1))
@@ -72,26 +101,70 @@ def tile_routed_moe_kernel(tc, xT, w1, w3, w2, gate, offs, out):
             )
 
         def load_w2(e):
-            raw_w2[e] = raw2.tile([P, 2, 4, N], F32, name="raw2")
+            raw_w2[e] = rawc.tile([P, 2, 4, N], F32, name="rawc") if ONE_RING else raw2.tile([P, 2, 4, N], F32, name="raw2")
             nc.sync.dma_start(out=raw_w2[e][:], in_=w2[e, :, :].rearrange("(g p j) n -> p g j n", g=2, j=4))
 
         def gather(gi, t):
+            if ALIAS_G1 and gi == 1:
+                if t % 2 == 0:
+                    pairs[t // 2] = alias.tile([P, 2, GROUP], F32, name="al%d" % (t // 2), align_bytes=64)
+                nc.vector.tensor_copy(
+                    out=pairs[t // 2][:, t % 2, :],
+                    in_=planes[t][:].indirect(offsets[:, GROUP * gi // 16 : GROUP * (gi + 1) // 16]),
+                )
+                return
             nc.vector.tensor_copy(
                 out=gathered[gi][:, t, :],
                 in_=planes[t][:].indirect(offsets[:, GROUP * gi // 16 : GROUP * (gi + 1) // 16]),
             )
 
         def copy_x(e):
+            if MERGE_X1 and e >= 2:
+                if e == 2:
+                    xg[2] = keep.tile([P, GROUP, 4], BF16, name="xg23", align_bytes=64)
+                    nc.scalar.copy(
+                        out=xg[2][:].rearrange("p (c i) t -> p c t i", i=4),
+                        in_=gathered[1][:].rearrange("p t (c i) -> p c t i", i=4),
+                    )
+                return
             col0 = e * C % GROUP
             xg[e] = keep.tile([P, C, 4], BF16, name="xg%d" % e, align_bytes=64)
-            nc.scalar.copy(
+            if ALIAS_G1 and e >= 2:
+                for h in range(2):
+                    nc.vector.tensor_copy(
+                        out=xg[e][:].rearrange("p (c i) t -> p c t i", i=4)[:, :, 2 * h : 2 * h + 2, :],
+                        in_=pairs[h][:, :, col0 : col0 + C].rearrange("p t (c i) -> p c t i", i=4),
+                    )
+                return
+            if GPS_X:
+                nc.gpsimd.tensor_scalar(
+                    out=xg[e][:],
+                    in0=gathered[e * C // GROUP][:, :, col0 : col0 + C].rearrange("p t c -> p c t"),
+                    scalar1=1.0,
+                    scalar2=0.0,
+                    op0=MULT,
+                    op1=ADD,
+                )
+                return
+            (nc.vector.tensor_copy if X_ON_V else nc.scalar.copy)(
                 out=xg[e][:].rearrange("p (c i) t -> p c t i", i=4),
                 in_=gathered[e * C // GROUP][:, :, col0 : col0 + C].rearrange("p t (c i) -> p c t i", i=4),
             )
 
         def quantise_x(e):
+            if MERGE_X1 and e >= 2:
+                if e == 2:
+                    xc = keep.tile([P, GROUP], U32, name="xc23", align_bytes=64)
+                    xs = keep.tile([P, GROUP], U8, name="xs23", align_bytes=64)
+                    nc.vector.quantize_mx(
+                        out=xc[:].bitcast(FP8X4), scales=xs[:], in_=xg[2][:].rearrange("p n t -> p (n t)")
+                    )
+                    for f in (2, 3):
+                        x_codes[f], x_scales[f], x_col0[f] = xc, xs, C * (f - 2)
+                return
             x_codes[e] = keep.tile([P, C], U32, name="xc%d" % e, align_bytes=64)
             x_scales[e] = keep.tile([P, C], U8, name="xs%d" % e, align_bytes=64)
+            x_col0[e] = 0
             nc.vector.quantize_mx(
                 out=x_codes[e][:].bitcast(FP8X4), scales=x_scales[e][:], in_=xg[e][:].rearrange("p n t -> p (n t)")
             )
@@ -102,7 +175,10 @@ def tile_routed_moe_kernel(tc, xT, w1, w3, w2, gate, offs, out):
             return dst, src
 
         def copy_chunk_scalar(m, u, vector_t):
-            grouped[m, u] = stage13.tile([P, 4 * HC], BF16, name="grouped13", align_bytes=64)
+            if ALIAS_G1 and u == 0:
+                grouped[m, u] = alias.tile([P, 4 * HC], BF16, name="al%d" % "ab".index(m), align_bytes=64)
+            else:
+                grouped[m, u] = stage13.tile([P, 4 * HC], BF16, name="grouped13", align_bytes=64)
             dst, src = views(m, u, 0, 4 - vector_t)
             nc.scalar.copy(out=dst, in_=src)
 
@@ -118,8 +194,15 @@ def tile_routed_moe_kernel(tc, xT, w1, w3, w2, gate, offs, out):
 
         def copy_w2(e):
             grouped_w2[e] = stage2.tile([P, 2, N, 4], BF16, name="grouped2", align_bytes=64)
-            for g in range(2):
+            on_scalar = (W2_LAST_ON_S and e == E - 1) or e in W2_ON_S
+            if MERGE_W2 and not on_scalar:
                 nc.vector.tensor_copy(
+                    out=grouped_w2[e][:].rearrange("p g (c i) j -> p g c j i", i=4),
+                    in_=raw_w2[e][:].rearrange("p g j (c i) -> p g c j i", i=4),
+                )
+                return
+            for g in range(2):
+                (nc.scalar.copy if on_scalar else nc.vector.tensor_copy)(
                     out=grouped_w2[e][:, g, :, :].rearrange("p (c i) j -> p c j i", i=4),
                     in_=raw_w2[e][:, g, :, :].rearrange("p j (c i) -> p c j i", i=4),
                 )
@@ -144,8 +227,8 @@ def tile_routed_moe_kernel(tc, xT, w1, w3, w2, gate, offs, out):
                             out=banks[m, u, s][:, t, :],
                             lhsT=codes[m, u][:, P * t : P * (t + 1)].bitcast(FP8X4),
                             lhsT_scale=scales[m, u][:, P * t : P * (t + 1)],
-                            rhs=x_codes[e][:, HALF * s : HALF * (s + 1)].bitcast(FP8X4),
-                            rhs_scale=x_scales[e][:, HALF * s : HALF * (s + 1)],
+                            rhs=x_codes[e][:, x_col0[e] + HALF * s : x_col0[e] + HALF * (s + 1)].bitcast(FP8X4),
+                            rhs_scale=x_scales[e][:, x_col0[e] + HALF * s : x_col0[e] + HALF * (s + 1)],
                             start=True,
                             stop=True,
                         )
@@ -157,6 +240,8 @@ def tile_routed_moe_kernel(tc, xT, w1, w3, w2, gate, offs, out):
             for s in range(2):
                 gelus[u, s] = gel.tile([P, HALF, 4], F32, name="ga")
                 nc.scalar.activation(out=gelus[u, s][:], in_=banks["a", u, s][:].rearrange("p t n -> p n t"), func=GELU)
+            if W2_LAST_ON_S and u == STAGES - 1:
+                copy_w2(E - 1)
             for s in range(2):
                 nc.vector.tensor_tensor(
                     out=hidden[e][:, s, hc, :, :],
@@ -198,38 +283,93 @@ def tile_routed_moe_kernel(tc, xT, w1, w3, w2, gate, offs, out):
             nc.vector.tensor_tensor(
                 out=windows[nb][:].indirect(offsets[:, first // 16 : last // 16]),
                 in0=ys[e, lo][:, nb, :, :].rearrange("p s n -> p (s n)"),
-                in1=gates[nb][:, first:last],
+                in1=gate_of(e, nb, lo, hi),
                 op=MULT,
             )
 
+        if PLANES_FIRST:
+            for c in range(4):
+                load_plane(c)
         for c in range(4):
-            load_plane(c)
+            if not PLANES_FIRST:
+                load_plane(c)
             load_chunk("ab"[c % 2], c // 2)
-        load_w2(0)
-        load_chunk("a", 2)
-        load_chunk("b", 2)
-        load_gates()
-        load_chunk("a", 3)
-        load_chunk("b", 3)
-        load_w2(1)
+        if LOADS3:
+            load_chunk("a", 2)
+            load_chunk("b", 2)
+            load_w2(0)
+            load_gate(0)
+            load_chunk("a", 3)
+            load_chunk("b", 3)
+        else:
+            load_w2(0)
+            load_chunk("a", 2)
+            load_chunk("b", 2)
+            load_gates()
+            load_chunk("a", 3)
+            load_chunk("b", 3)
+            load_w2(1)
 
-        gather(0, 0)
-        gather(1, 0)
-        for k in range(STAGES):
+        if PLANES_FIRST:
+            for t in range(4):
+                gather(0, t)
+            copy_x(0)
+            quantise_x(0)
+        else:
+            gather(0, 0)
+            gather(1, 0)
+        if CUT:
+            for nb in range(2):
+                nc.gpsimd.memset(windows[nb][:], 0.0)
+        for k in range(STAGES if PLANES_FIRST else 0):
+            e, hc = k // 2, k % 2
+            copy_chunk_scalar("a", k, 0)
+            quantise_chunk("a", k)
+            copy_chunk_scalar("b", k, VECTOR_T[k])
+            copy_chunk_vector("b", k, VECTOR_T[k])
+            quantise_chunk("b", k)
+            first_layer(k)
+            if k + AHEAD < STAGES:
+                load_chunk("a", k + AHEAD)
+                load_chunk("b", k + AHEAD)
+                if hc == 1:
+                    load_w2((k + AHEAD) // 2)
+            if k >= 2 and hc == 0:
+                copy_y(e - 1, 0, 2)
+            if hc == 1 and e + 1 < E:
+                copy_x(e + 1)
+            if hc == 1 and not (W2_LAST_ON_S and e == E - 1):
+                quantise_w2(e)
+            if k >= 2:
+                scatter((k - 2) // 2, 0, 2, hc)
+            hidden_values(k)
+            if hc == 1 and e + 1 < E:
+                second_layer(e, 0, 2)
+            if hc == 0 and not (W2_LAST_ON_S and e == E - 1):
+                copy_w2(e)
+            if hc == 1 and e + 1 < E:
+                quantise_x(e + 1)
+            if k == G1_AT:
+                for t in range(4):
+                    gather(1, t)
+        for k in range(0 if PLANES_FIRST else (CUT or STAGES)):
             e, hc = k // 2, k % 2
             copy_chunk_scalar("a", k, 0)
             if k < 2:
                 gather(0, 2 * k + 1)
+            if k == 1 and X0_SOON:
+                copy_x(0)
+                quantise_x(0)
             quantise_chunk("a", k)
             if k < 2:
                 gather(1, 2 * k + 1)
-            if k == 1:
+            if k == 1 and not X0_SOON:
                 copy_x(0)
             copy_chunk_scalar("b", k, VECTOR_T[k])
             if k == 0:
                 gather(0, 2)
             copy_chunk_vector("b", k, VECTOR_T[k])
-            if k == 1:
+            if k == 1 and not X0_SOON:
                 quantise_x(0)
             quantise_chunk("b", k)
             if k == 0:
@@ -241,15 +381,18 @@ def tile_routed_moe_kernel(tc, xT, w1, w3, w2, gate, offs, out):
             if k + AHEAD < STAGES:
                 load_chunk("a", k + AHEAD)
                 load_chunk("b", k + AHEAD)
-                if hc == 1:
+                if LOADS3 and k != 1:
+                    load_w2((k + 2) // 2 + (1 if k == 3 else 0))
+                    load_gate((k + 2) // 2 + (1 if k == 3 else 0))
+                if hc == 1 and not LOADS3:
                     load_w2((k + AHEAD) // 2)
             if k >= 2 and hc == 0:
                 copy_y(e - 1, 0, 2)
-            if hc == 1 and e + 1 < E:
+            if hc == 1 and e + 1 < E and not (X_EARLY and e >= 1):
                 copy_x(e + 1)
             if k == 1:
                 copy_w2(0)
-            if hc == 1:
+            if hc == 1 and not (W2_LAST_ON_S and e == E - 1):
                 quantise_w2(e)
             if k >= 2:
                 scatter((k - 2) // 2, 0, 2, hc)
@@ -259,17 +402,60 @@ def tile_routed_moe_kernel(tc, xT, w1, w3, w2, gate, offs, out):
                 hidden_values(k)
             if hc == 1 and e + 1 < E:
                 second_layer(e, 0, 2)
-            if hc == 0 and k >= 2:
+            if hc == 0 and k >= 2 and not (W2_LAST_ON_S and e == E - 1):
                 copy_w2(e)
             if hc == 1 and e + 1 < E:
                 quantise_x(e + 1)
-        for s in range(2):
-            second_layer(E - 1, s, s + 1)
-        for s in range(2):
-            copy_y(E - 1, s, s + 1)
-        for s in range(2):
+            if X_EARLY and k == 1:
+                copy_x(2)
+                copy_x(3)
+        if W2_LAST_ON_S:
+            quantise_w2(E - 1)
+        if CUT:
             for nb in range(2):
-                scatter(E - 1, s, s + 1, nb)
+                nc.sync.dma_start(out=out[P * nb : P * (nb + 1), :], in_=windows[nb][:])
+        elif TAIL_NB:
+            e = E - 1
+            tail_codes, tail_scales = {}, {}
+            for s in range(2):
+                tail_codes[s] = hid.tile([P, 2, HALF], U32, name="hcodes", align_bytes=64)
+                tail_scales[s] = hid.tile([P, 2, HALF], U8, name="hscales", align_bytes=64)
+                nc.vector.quantize_mx(
+                    out=tail_codes[s][:].rearrange("p g n -> p (g n)").bitcast(FP8X4),
+                    scales=tail_scales[s][:].rearrange("p g n -> p (g n)"),
+                    in_=hidden[e][:, s, :, :, :].rearrange("p g n t -> p (g n t)"),
+                )
+            c2, s2 = q_w2[e]
+            for nb in range(2):
+                py = psum_y.tile([P, 2, HALF], F32, name="py")
+                for s in range(2):
+                    for g in range(2):
+                        nc.tensor.matmul_mx(
+                            out=py[:, s, :],
+                            lhsT=c2[:, g, P * nb : P * (nb + 1)].bitcast(FP8X4),
+                            lhsT_scale=s2[:, g, P * nb : P * (nb + 1)],
+                            rhs=tail_codes[s][:, g, :].bitcast(FP8X4),
+                            rhs_scale=tail_scales[s][:, g, :],
+                            start=(g == 0),
+                            stop=(g == 1),
+                        )
+                y_nb = hid.tile([P, C], F32, name="y")
+                nc.scalar.copy(out=y_nb[:], in_=py[:].rearrange("p s n -> p (s n)"))
+                nc.vector.tensor_tensor(
+                    out=windows[nb][:].indirect(offsets[:, C * e // 16 : C * (e + 1) // 16]),
+                    in0=y_nb[:],
+                    in1=gate_of(e, nb, 0, 2),
+                    op=MULT,
+                )
+                nc.sync.dma_start(out=out[P * nb : P * (nb + 1), :], in_=windows[nb][:])
+        else:
+            for s in range(2):
+                second_layer(E - 1, s, s + 1)
+            for s in range(2):
+                copy_y(E - 1, s, s + 1)
+            for s in range(2):
+                for nb in range(2):
+                    scatter(E - 1, s, s + 1, nb)
 
-        for nb in range(2):
-            nc.sync.dma_start(out=out[P * nb : P * (nb + 1), :], in_=windows[nb][:])
+            for nb in range(2):
+                nc.sync.dma_start(out=out[P * nb : P * (nb + 1), :], in_=windows[nb][:])

@@ -12,6 +12,7 @@ U16 = mybir.dt.uint16
 U8 = mybir.dt.uint8
 FP8X4 = mybir.dt.float8_e4m3fn_x4
 GELU = mybir.ActivationFunctionType.Gelu_apprx_tanh
+COPY = mybir.ActivationFunctionType.Copy
 MULT = mybir.AluOpType.mult
 ADD = mybir.AluOpType.add
 
@@ -26,13 +27,22 @@ MERGE_W2 = True
 W2_ON_S = ()
 X0_SOON = False
 W2_LAST_ON_S = False
+TAIL_G = False
 TAIL_NB = False
 CUT = 0
+W0_LATE = False
+W_AT = {0: (1,), 2: (2,), 3: (3,)}
 LOADS3 = True
 ONE_RING = False
 ALIAS_G1 = False
 PLANES_FIRST = False
 G1_AT = 0
+WARM = ()
+F_GROUPS = ()
+SPLIT_LAST = False
+X_V_EXPERTS = (0, 1, 2, 3)
+HOLD_SC = True
+X_PAIRS = False
 X_ON_V = True
 X_EARLY = False
 GPS_X = False
@@ -52,6 +62,8 @@ def tile_routed_moe_kernel(tc, xT, w1, w3, w2, gate, offs, out):
         hid = ctx.enter_context(tc.tile_pool(name="hid", bufs=2))
         gel = ctx.enter_context(tc.tile_pool(name="gel", bufs=4))
         psum_ab = ctx.enter_context(tc.psum_pool(name="psum_ab", bufs=3))
+        psum_a2 = ctx.enter_context(tc.psum_pool(name="psum_a2", bufs=2)) if WARM else psum_ab
+        psum_w = ctx.enter_context(tc.psum_pool(name="psum_w", bufs=1)) if WARM else psum_ab
         psum_y = ctx.enter_context(tc.psum_pool(name="psum_y", bufs=2))
 
         offsets = lists.tile([P, T // 16], U16, name="offsets")
@@ -104,7 +116,22 @@ def tile_routed_moe_kernel(tc, xT, w1, w3, w2, gate, offs, out):
             raw_w2[e] = rawc.tile([P, 2, 4, N], F32, name="rawc") if ONE_RING else raw2.tile([P, 2, 4, N], F32, name="raw2")
             nc.sync.dma_start(out=raw_w2[e][:], in_=w2[e, :, :].rearrange("(g p j) n -> p g j n", g=2, j=4))
 
+        planes16 = {}
+
         def gather(gi, t):
+            if gi in F_GROUPS and t < 2:
+                if t not in planes16:
+                    planes16[t] = keep.tile([P, T], BF16, name="plane16_%d" % t)
+                    nc.scalar.copy(out=planes16[t][:], in_=planes[t][:])
+                for e in (2 * gi, 2 * gi + 1):
+                    if e not in xg:
+                        xg[e] = keep.tile([P, C, 4], BF16, name="xg%d" % e, align_bytes=64)
+                    nc.scalar.activation(
+                        out=xg[e][:, :, t],
+                        in_=planes16[t][:].indirect(offsets[:, C * e // 16 : C * (e + 1) // 16]),
+                        func=COPY,
+                    )
+                return
             if ALIAS_G1 and gi == 1:
                 if t % 2 == 0:
                     pairs[t // 2] = alias.tile([P, 2, GROUP], F32, name="al%d" % (t // 2), align_bytes=64)
@@ -119,6 +146,14 @@ def tile_routed_moe_kernel(tc, xT, w1, w3, w2, gate, offs, out):
             )
 
         def copy_x(e):
+            if X_PAIRS:
+                if e % 2 == 0:
+                    xg[e] = keep.tile([P, GROUP, 4], BF16, name="xgp%d" % e, align_bytes=64)
+                    nc.vector.tensor_copy(
+                        out=xg[e][:].rearrange("p (c i) t -> p c t i", i=4),
+                        in_=gathered[e // 2][:].rearrange("p t (c i) -> p c t i", i=4),
+                    )
+                return
             if MERGE_X1 and e >= 2:
                 if e == 2:
                     xg[2] = keep.tile([P, GROUP, 4], BF16, name="xg23", align_bytes=64)
@@ -128,6 +163,12 @@ def tile_routed_moe_kernel(tc, xT, w1, w3, w2, gate, offs, out):
                     )
                 return
             col0 = e * C % GROUP
+            if e // 2 in F_GROUPS:
+                nc.vector.tensor_copy(
+                    out=xg[e][:].rearrange("p (c i) t -> p c t i", i=4)[:, :, 2:4, :],
+                    in_=gathered[e // 2][:, 2:4, col0 : col0 + C].rearrange("p t (c i) -> p c t i", i=4),
+                )
+                return
             xg[e] = keep.tile([P, C, 4], BF16, name="xg%d" % e, align_bytes=64)
             if ALIAS_G1 and e >= 2:
                 for h in range(2):
@@ -146,12 +187,22 @@ def tile_routed_moe_kernel(tc, xT, w1, w3, w2, gate, offs, out):
                     op1=ADD,
                 )
                 return
-            (nc.vector.tensor_copy if X_ON_V else nc.scalar.copy)(
+            (nc.vector.tensor_copy if X_ON_V and e in X_V_EXPERTS else nc.scalar.copy)(
                 out=xg[e][:].rearrange("p (c i) t -> p c t i", i=4),
                 in_=gathered[e * C // GROUP][:, :, col0 : col0 + C].rearrange("p t (c i) -> p c t i", i=4),
             )
 
         def quantise_x(e):
+            if X_PAIRS:
+                if e % 2 == 0:
+                    xc = keep.tile([P, GROUP], U32, name="xcp%d" % e, align_bytes=64)
+                    xs = keep.tile([P, GROUP], U8, name="xsp%d" % e, align_bytes=64)
+                    nc.vector.quantize_mx(
+                        out=xc[:].bitcast(FP8X4), scales=xs[:], in_=xg[e][:].rearrange("p n t -> p (n t)")
+                    )
+                    for f in (e, e + 1):
+                        x_codes[f], x_scales[f], x_col0[f] = xc, xs, C * (f - e)
+                return
             if MERGE_X1 and e >= 2:
                 if e == 2:
                     xc = keep.tile([P, GROUP], U32, name="xc23", align_bytes=64)
@@ -173,6 +224,19 @@ def tile_routed_moe_kernel(tc, xT, w1, w3, w2, gate, offs, out):
             dst = grouped[m, u][:, HC * t0 : HC * t1].rearrange("p (t i j) -> p i j t", t=t1 - t0, j=4)
             src = raw[m, u][:].rearrange("p j (i t) -> p i j t", t=4)[:, :, :, t0:t1]
             return dst, src
+
+        def split_chunk(m, u):
+            grouped[m, u] = stage13.tile([P, 4 * HC], BF16, name="grouped13", align_bytes=64)
+            codes[m, u] = wq.tile([P, HC], U32, name="c" + m, align_bytes=64)
+            scales[m, u] = wq.tile([P, HC], U8, name="s" + m, align_bytes=64)
+            for half in range(2):
+                dst, src = views(m, u, 2 * half, 2 * half + 2)
+                nc.scalar.copy(out=dst, in_=src)
+                nc.vector.quantize_mx(
+                    out=codes[m, u][:, 2 * P * half : 2 * P * (half + 1)].bitcast(FP8X4),
+                    scales=scales[m, u][:, 2 * P * half : 2 * P * (half + 1)],
+                    in_=grouped[m, u][:, 2 * HC * half : 2 * HC * (half + 1)],
+                )
 
         def copy_chunk_scalar(m, u, vector_t):
             if ALIAS_G1 and u == 0:
@@ -217,12 +281,19 @@ def tile_routed_moe_kernel(tc, xT, w1, w3, w2, gate, offs, out):
             )
             q_w2[e] = (c2, s2)
 
+        def keep_warm(source, count):
+            for j in range(count):
+                idle_bank = psum_w.tile([P, 512], F32, name="pw")
+                nc.tensor.matmul(idle_bank[:], lhsT=source[:, 0:P], rhs=source[:, 512 * j : 512 * (j + 1)], start=True, stop=True)
+
         def first_layer(u):
             e = u // 2
             for m in ("a", "b"):
-                for s in range(2):
-                    banks[m, u, s] = psum_ab.tile([P, 4, HALF], F32, name="p" + m)
-                    for t in range(4):
+                split = SPLIT_LAST and m == "b" and u == STAGES - 1
+                for s, ts in ((0, (0, 1)), (1, (0, 1)), (0, (2, 3)), (1, (2, 3))) if split else ((0, range(4)), (1, range(4))):
+                    if ts[0] == 0:
+                        banks[m, u, s] = (psum_a2 if WARM and m == "a" else psum_ab).tile([P, 4, HALF], F32, name="p" + m)
+                    for t in ts:
                         nc.tensor.matmul_mx(
                             out=banks[m, u, s][:, t, :],
                             lhsT=codes[m, u][:, P * t : P * (t + 1)].bitcast(FP8X4),
@@ -237,17 +308,49 @@ def tile_routed_moe_kernel(tc, xT, w1, w3, w2, gate, offs, out):
             e, hc = u // 2, u % 2
             if hc == 0:
                 hidden[e] = hid.tile([P, 2, 2, HALF, 4], BF16, name="hg", align_bytes=64)
+            last = TAIL_G and e == E - 1
             for s in range(2):
-                gelus[u, s] = gel.tile([P, HALF, 4], F32, name="ga")
+                if HOLD_SC and u == STAGES - 1 and s == 1:
+                    gelus[u, s] = alias.tile([P, HALF, 4], F32, name="held")
+                else:
+                    gelus[u, s] = gel.tile([P, HALF, 4], F32, name="ga")
                 nc.scalar.activation(out=gelus[u, s][:], in_=banks["a", u, s][:].rearrange("p t n -> p n t"), func=GELU)
             if W2_LAST_ON_S and u == STAGES - 1:
                 copy_w2(E - 1)
             for s in range(2):
                 nc.vector.tensor_tensor(
-                    out=hidden[e][:, s, hc, :, :],
+                    out=hidden[e][:, hc, s, :, :] if last else hidden[e][:, s, hc, :, :],
                     in0=banks["b", u, s][:].rearrange("p t n -> p n t"),
                     in1=gelus[u, s][:],
                     op=MULT,
+                )
+                if WARM and u == STAGES - 1:
+                    keep_warm(hidden[e][:, s, :, :, :].rearrange("p g n t -> p (g n t)"), WARM[2])
+
+        tail_sums = {}
+        held_y = {}
+
+        def tail_pass(g):
+            e = E - 1
+            t_codes = hid.tile([P, C], U32, name="tcodes", align_bytes=64)
+            t_scales = hid.tile([P, C], U8, name="tscales", align_bytes=64)
+            nc.vector.quantize_mx(
+                out=t_codes[:].bitcast(FP8X4),
+                scales=t_scales[:],
+                in_=hidden[e][:, g, :, :, :].rearrange("p s n t -> p (s n t)"),
+            )
+            c2, s2 = q_w2[e]
+            for nb in range(2):
+                if g == 0:
+                    tail_sums[nb] = psum_y.tile([P, C], F32, name="py")
+                nc.tensor.matmul_mx(
+                    out=tail_sums[nb][:],
+                    lhsT=c2[:, g, P * nb : P * (nb + 1)].bitcast(FP8X4),
+                    lhsT_scale=s2[:, g, P * nb : P * (nb + 1)],
+                    rhs=t_codes[:].bitcast(FP8X4),
+                    rhs_scale=t_scales[:],
+                    start=(g == 0),
+                    stop=(g == 1),
                 )
 
         def second_layer(e, lo, hi):
@@ -275,14 +378,22 @@ def tile_routed_moe_kernel(tc, xT, w1, w3, w2, gate, offs, out):
                         )
 
         def copy_y(e, lo, hi):
+            if HOLD_SC and e == E - 2:
+                held_y[0] = hid.tile([P, 2, HALF], F32, name="y")
+                nc.scalar.copy(out=held_y[0][:], in_=sums[e, lo][:, :, 0, :])
+                return
             ys[e, lo] = hid.tile([P, 2, hi - lo, HALF], F32, name="y")
             nc.scalar.copy(out=ys[e, lo][:], in_=sums[e, lo][:].rearrange("p s b n -> p b s n"))
+
+        def copy_held_y():
+            held_y[1] = alias.tile([P, 2, HALF], F32, name="held")
+            nc.scalar.copy(out=held_y[1][:], in_=sums[E - 2, 0][:, :, 1, :])
 
         def scatter(e, lo, hi, nb):
             first, last = C * e + HALF * lo, C * e + HALF * hi
             nc.vector.tensor_tensor(
                 out=windows[nb][:].indirect(offsets[:, first // 16 : last // 16]),
-                in0=ys[e, lo][:, nb, :, :].rearrange("p s n -> p (s n)"),
+                in0=(held_y[nb][:] if HOLD_SC and e == E - 2 else ys[e, lo][:, nb, :, :]).rearrange("p s n -> p (s n)"),
                 in1=gate_of(e, nb, lo, hi),
                 op=MULT,
             )
@@ -297,10 +408,14 @@ def tile_routed_moe_kernel(tc, xT, w1, w3, w2, gate, offs, out):
         if LOADS3:
             load_chunk("a", 2)
             load_chunk("b", 2)
-            load_w2(0)
-            load_gate(0)
+            if not W0_LATE:
+                load_w2(0)
+                load_gate(0)
             load_chunk("a", 3)
             load_chunk("b", 3)
+            if W0_LATE:
+                load_w2(0)
+                load_gate(0)
         else:
             load_w2(0)
             load_chunk("a", 2)
@@ -355,6 +470,8 @@ def tile_routed_moe_kernel(tc, xT, w1, w3, w2, gate, offs, out):
         for k in range(0 if PLANES_FIRST else (CUT or STAGES)):
             e, hc = k // 2, k % 2
             copy_chunk_scalar("a", k, 0)
+            if WARM and k == STAGES - 1:
+                keep_warm(grouped["a", k], WARM[0])
             if k < 2:
                 gather(0, 2 * k + 1)
             if k == 1 and X0_SOON:
@@ -365,13 +482,19 @@ def tile_routed_moe_kernel(tc, xT, w1, w3, w2, gate, offs, out):
                 gather(1, 2 * k + 1)
             if k == 1 and not X0_SOON:
                 copy_x(0)
-            copy_chunk_scalar("b", k, VECTOR_T[k])
+            if SPLIT_LAST and k == STAGES - 1:
+                split_chunk("b", k)
+            else:
+                copy_chunk_scalar("b", k, VECTOR_T[k])
+            if WARM and k == STAGES - 1:
+                keep_warm(grouped["b", k], WARM[1])
             if k == 0:
                 gather(0, 2)
             copy_chunk_vector("b", k, VECTOR_T[k])
             if k == 1 and not X0_SOON:
                 quantise_x(0)
-            quantise_chunk("b", k)
+            if not (SPLIT_LAST and k == STAGES - 1):
+                quantise_chunk("b", k)
             if k == 0:
                 gather(1, 2)
             if k == 1:
@@ -381,9 +504,10 @@ def tile_routed_moe_kernel(tc, xT, w1, w3, w2, gate, offs, out):
             if k + AHEAD < STAGES:
                 load_chunk("a", k + AHEAD)
                 load_chunk("b", k + AHEAD)
-                if LOADS3 and k != 1:
-                    load_w2((k + 2) // 2 + (1 if k == 3 else 0))
-                    load_gate((k + 2) // 2 + (1 if k == 3 else 0))
+                if LOADS3 and k in W_AT:
+                    for f in W_AT[k]:
+                        load_w2(f)
+                        load_gate(f)
                 if hc == 1 and not LOADS3:
                     load_w2((k + AHEAD) // 2)
             if k >= 2 and hc == 0:
@@ -394,12 +518,15 @@ def tile_routed_moe_kernel(tc, xT, w1, w3, w2, gate, offs, out):
                 copy_w2(0)
             if hc == 1 and not (W2_LAST_ON_S and e == E - 1):
                 quantise_w2(e)
-            if k >= 2:
+            if k >= 2 and not (HOLD_SC and k == STAGES - 1):
                 scatter((k - 2) // 2, 0, 2, hc)
             if k == 1:
                 hidden_values(0)
             if k >= 1:
                 hidden_values(k)
+            if HOLD_SC and k == STAGES - 1:
+                copy_held_y()
+                scatter(E - 2, 0, 2, 1)
             if hc == 1 and e + 1 < E:
                 second_layer(e, 0, 2)
             if hc == 0 and k >= 2 and not (W2_LAST_ON_S and e == E - 1):
@@ -413,6 +540,20 @@ def tile_routed_moe_kernel(tc, xT, w1, w3, w2, gate, offs, out):
             quantise_w2(E - 1)
         if CUT:
             for nb in range(2):
+                nc.sync.dma_start(out=out[P * nb : P * (nb + 1), :], in_=windows[nb][:])
+        elif TAIL_G:
+            e = E - 1
+            tail_pass(0)
+            tail_pass(1)
+            for nb in range(2):
+                y_nb = hid.tile([P, C], F32, name="y")
+                nc.scalar.copy(out=y_nb[:], in_=tail_sums[nb][:])
+                nc.vector.tensor_tensor(
+                    out=windows[nb][:].indirect(offsets[:, C * e // 16 : C * (e + 1) // 16]),
+                    in0=y_nb[:],
+                    in1=gate_of(e, nb, 0, 2),
+                    op=MULT,
+                )
                 nc.sync.dma_start(out=out[P * nb : P * (nb + 1), :], in_=windows[nb][:])
         elif TAIL_NB:
             e = E - 1

@@ -37,11 +37,16 @@ ONE_RING = False
 ALIAS_G1 = False
 PLANES_FIRST = False
 G1_AT = 0
+PB4 = True
+WARM_FROM = 0
 WARM = ()
 F_GROUPS = ()
 SPLIT_LAST = False
 X_V_EXPERTS = (0, 1, 2, 3)
+HOLD_HALF = True
 HOLD_SC = True
+WIDE_G = 1376
+B_FIRST = False
 X_PAIRS = False
 X_ON_V = True
 X_EARLY = False
@@ -61,9 +66,9 @@ def tile_routed_moe_kernel(tc, xT, w1, w3, w2, gate, offs, out):
         wq = ctx.enter_context(tc.tile_pool(name="wq", bufs=3))
         hid = ctx.enter_context(tc.tile_pool(name="hid", bufs=2))
         gel = ctx.enter_context(tc.tile_pool(name="gel", bufs=4))
-        psum_ab = ctx.enter_context(tc.psum_pool(name="psum_ab", bufs=3))
-        psum_a2 = ctx.enter_context(tc.psum_pool(name="psum_a2", bufs=2)) if WARM else psum_ab
-        psum_w = ctx.enter_context(tc.psum_pool(name="psum_w", bufs=1)) if WARM else psum_ab
+        psum_ab = ctx.enter_context(tc.psum_pool(name="psum_ab", bufs=4 if PB4 else 3))
+        psum_a2 = ctx.enter_context(tc.psum_pool(name="psum_a2", bufs=2)) if WARM or WARM_FROM or PB4 else psum_ab
+        psum_w = ctx.enter_context(tc.psum_pool(name="psum_w", bufs=1)) if WARM or WARM_FROM else psum_ab
         psum_y = ctx.enter_context(tc.psum_pool(name="psum_y", bufs=2))
 
         offsets = lists.tile([P, T // 16], U16, name="offsets")
@@ -75,13 +80,16 @@ def tile_routed_moe_kernel(tc, xT, w1, w3, w2, gate, offs, out):
         nc.scalar.activation(out=warmed[:], in_=warm[:], func=GELU)
 
         x_rows = xT.rearrange("(p t) n -> p t n", t=4)
-        planes = [keep.tile([P, T], F32, name="plane%d" % t) for t in range(4)]
+        planes = [keep.tile([P, WIDE_G or T], F32, name="plane%d" % t) for t in range(4)]
         if LOADS3:
             gates = [keep.tile([P, 2, C], F32, name="gate%d" % e) for e in range(E)]
         else:
             gates = [keep.tile([P, E * C], F32, name="gate%d" % nb) for nb in range(2)]
         windows = [keep.tile([P, T], F32, name="window%d" % nb) for nb in range(2)]
-        gathered = [keep.tile([P, 4, GROUP], F32, name="g4_%d" % gi) for gi in range(1 if ALIAS_G1 else E * C // GROUP)]
+        if WIDE_G:
+            gathered = [keep.tile([P, 4, E * C], F32, name="g4")]
+        else:
+            gathered = [keep.tile([P, 4, GROUP], F32, name="g4_%d" % gi) for gi in range(1 if ALIAS_G1 else E * C // GROUP)]
         alias = ctx.enter_context(tc.tile_pool(name="alias", bufs=1))
         pairs = {}
         sources = {"a": w1, "b": w3}
@@ -90,8 +98,11 @@ def tile_routed_moe_kernel(tc, xT, w1, w3, w2, gate, offs, out):
         xg, x_codes, x_scales, x_col0 = {}, {}, {}, {}
         banks, gelus, hidden, sums, ys = {}, {}, {}, {}, {}
 
+        def order_of(u):
+            return ("b", "a") if B_FIRST and u < STAGES - 1 else ("a", "b")
+
         def load_plane(t):
-            nc.sync.dma_start(out=planes[t][:], in_=x_rows[:, t, :])
+            nc.sync.dma_start(out=planes[t][:, 0:T], in_=x_rows[:, t, :])
 
         def load_gates():
             for nb in range(2):
@@ -119,6 +130,10 @@ def tile_routed_moe_kernel(tc, xT, w1, w3, w2, gate, offs, out):
         planes16 = {}
 
         def gather(gi, t):
+            if WIDE_G:
+                if gi == 0:
+                    nc.vector.tensor_copy(out=gathered[0][:, t, :], in_=planes[t][:].indirect(offsets[:]))
+                return
             if gi in F_GROUPS and t < 2:
                 if t not in planes16:
                     planes16[t] = keep.tile([P, T], BF16, name="plane16_%d" % t)
@@ -189,7 +204,9 @@ def tile_routed_moe_kernel(tc, xT, w1, w3, w2, gate, offs, out):
                 return
             (nc.vector.tensor_copy if X_ON_V and e in X_V_EXPERTS else nc.scalar.copy)(
                 out=xg[e][:].rearrange("p (c i) t -> p c t i", i=4),
-                in_=gathered[e * C // GROUP][:, :, col0 : col0 + C].rearrange("p t (c i) -> p c t i", i=4),
+                in_=(
+                    gathered[0][:, :, C * e : C * (e + 1)] if WIDE_G else gathered[e * C // GROUP][:, :, col0 : col0 + C]
+                ).rearrange("p t (c i) -> p c t i", i=4),
             )
 
         def quantise_x(e):
@@ -245,6 +262,8 @@ def tile_routed_moe_kernel(tc, xT, w1, w3, w2, gate, offs, out):
                 grouped[m, u] = stage13.tile([P, 4 * HC], BF16, name="grouped13", align_bytes=64)
             dst, src = views(m, u, 0, 4 - vector_t)
             nc.scalar.copy(out=dst, in_=src)
+            if WARM_FROM and u >= WARM_FROM:
+                keep_warm(grouped[m, u], 1)
 
         def copy_chunk_vector(m, u, vector_t):
             if vector_t > 0:
@@ -288,11 +307,11 @@ def tile_routed_moe_kernel(tc, xT, w1, w3, w2, gate, offs, out):
 
         def first_layer(u):
             e = u // 2
-            for m in ("a", "b"):
+            for m in order_of(u):
                 split = SPLIT_LAST and m == "b" and u == STAGES - 1
                 for s, ts in ((0, (0, 1)), (1, (0, 1)), (0, (2, 3)), (1, (2, 3))) if split else ((0, range(4)), (1, range(4))):
                     if ts[0] == 0:
-                        banks[m, u, s] = (psum_a2 if WARM and m == "a" else psum_ab).tile([P, 4, HALF], F32, name="p" + m)
+                        banks[m, u, s] = (psum_a2 if (WARM or WARM_FROM or PB4) and m == "a" else psum_ab).tile([P, 4, HALF], F32, name="p" + m)
                     for t in ts:
                         nc.tensor.matmul_mx(
                             out=banks[m, u, s][:, t, :],
@@ -379,6 +398,11 @@ def tile_routed_moe_kernel(tc, xT, w1, w3, w2, gate, offs, out):
 
         def copy_y(e, lo, hi):
             if HOLD_SC and e == E - 2:
+                if HOLD_HALF:
+                    held_y[0] = hid.tile([P, 3, HALF], F32, name="y")
+                    nc.scalar.copy(out=held_y[0][:, 0:2, :], in_=sums[e, lo][:, :, 0, :])
+                    nc.scalar.copy(out=held_y[0][:, 2, :], in_=sums[e, lo][:, 0, 1, :])
+                    return
                 held_y[0] = hid.tile([P, 2, HALF], F32, name="y")
                 nc.scalar.copy(out=held_y[0][:], in_=sums[e, lo][:, :, 0, :])
                 return
@@ -386,14 +410,30 @@ def tile_routed_moe_kernel(tc, xT, w1, w3, w2, gate, offs, out):
             nc.scalar.copy(out=ys[e, lo][:], in_=sums[e, lo][:].rearrange("p s b n -> p b s n"))
 
         def copy_held_y():
+            if HOLD_HALF:
+                held_y[1] = alias.tile([P, HALF], F32, name="held")
+                nc.scalar.copy(out=held_y[1][:], in_=sums[E - 2, 0][:, 1, 1, :])
+                return
             held_y[1] = alias.tile([P, 2, HALF], F32, name="held")
             nc.scalar.copy(out=held_y[1][:], in_=sums[E - 2, 0][:, :, 1, :])
+
+        def scatter_held(part):
+            e = E - 2
+            first = C * e + HALF * part
+            nc.vector.tensor_tensor(
+                out=windows[1][:].indirect(offsets[:, first // 16 : (first + HALF) // 16]),
+                in0=held_y[0][:, 2, :] if part == 0 else held_y[1][:],
+                in1=gate_of(e, 1, part, part + 1),
+                op=MULT,
+            )
 
         def scatter(e, lo, hi, nb):
             first, last = C * e + HALF * lo, C * e + HALF * hi
             nc.vector.tensor_tensor(
                 out=windows[nb][:].indirect(offsets[:, first // 16 : last // 16]),
-                in0=(held_y[nb][:] if HOLD_SC and e == E - 2 else ys[e, lo][:, nb, :, :]).rearrange("p s n -> p (s n)"),
+                in0=(
+                    (held_y[0][:, 0:2, :] if HOLD_HALF else held_y[nb][:]) if HOLD_SC and e == E - 2 else ys[e, lo][:, nb, :, :]
+                ).rearrange("p s n -> p (s n)"),
                 in1=gate_of(e, nb, lo, hi),
                 op=MULT,
             )
@@ -404,15 +444,15 @@ def tile_routed_moe_kernel(tc, xT, w1, w3, w2, gate, offs, out):
         for c in range(4):
             if not PLANES_FIRST:
                 load_plane(c)
-            load_chunk("ab"[c % 2], c // 2)
+            load_chunk(order_of(c // 2)[c % 2], c // 2)
         if LOADS3:
-            load_chunk("a", 2)
-            load_chunk("b", 2)
+            for m in order_of(2):
+                load_chunk(m, 2)
             if not W0_LATE:
                 load_w2(0)
                 load_gate(0)
-            load_chunk("a", 3)
-            load_chunk("b", 3)
+            for m in order_of(3):
+                load_chunk(m, 3)
             if W0_LATE:
                 load_w2(0)
                 load_gate(0)
@@ -447,7 +487,11 @@ def tile_routed_moe_kernel(tc, xT, w1, w3, w2, gate, offs, out):
             if k + AHEAD < STAGES:
                 load_chunk("a", k + AHEAD)
                 load_chunk("b", k + AHEAD)
-                if hc == 1:
+                if LOADS3 and k in W_AT:
+                    for f in W_AT[k]:
+                        load_w2(f)
+                        load_gate(f)
+                if hc == 1 and not LOADS3:
                     load_w2((k + AHEAD) // 2)
             if k >= 2 and hc == 0:
                 copy_y(e - 1, 0, 2)
@@ -455,9 +499,17 @@ def tile_routed_moe_kernel(tc, xT, w1, w3, w2, gate, offs, out):
                 copy_x(e + 1)
             if hc == 1 and not (W2_LAST_ON_S and e == E - 1):
                 quantise_w2(e)
-            if k >= 2:
+            if k >= 2 and not (HOLD_SC and k == STAGES - 1):
                 scatter((k - 2) // 2, 0, 2, hc)
+            if HOLD_HALF and k == STAGES - 1:
+                scatter_held(0)
             hidden_values(k)
+            if HOLD_SC and k == STAGES - 1:
+                copy_held_y()
+                if HOLD_HALF:
+                    scatter_held(1)
+                else:
+                    scatter(E - 2, 0, 2, 1)
             if hc == 1 and e + 1 < E:
                 second_layer(e, 0, 2)
             if hc == 0 and not (W2_LAST_ON_S and e == E - 1):
@@ -469,7 +521,8 @@ def tile_routed_moe_kernel(tc, xT, w1, w3, w2, gate, offs, out):
                     gather(1, t)
         for k in range(0 if PLANES_FIRST else (CUT or STAGES)):
             e, hc = k // 2, k % 2
-            copy_chunk_scalar("a", k, 0)
+            m1, m2 = order_of(k)
+            copy_chunk_scalar(m1, k, 0)
             if WARM and k == STAGES - 1:
                 keep_warm(grouped["a", k], WARM[0])
             if k < 2:
@@ -477,7 +530,7 @@ def tile_routed_moe_kernel(tc, xT, w1, w3, w2, gate, offs, out):
             if k == 1 and X0_SOON:
                 copy_x(0)
                 quantise_x(0)
-            quantise_chunk("a", k)
+            quantise_chunk(m1, k)
             if k < 2:
                 gather(1, 2 * k + 1)
             if k == 1 and not X0_SOON:
@@ -485,16 +538,16 @@ def tile_routed_moe_kernel(tc, xT, w1, w3, w2, gate, offs, out):
             if SPLIT_LAST and k == STAGES - 1:
                 split_chunk("b", k)
             else:
-                copy_chunk_scalar("b", k, VECTOR_T[k])
+                copy_chunk_scalar(m2, k, VECTOR_T[k])
             if WARM and k == STAGES - 1:
                 keep_warm(grouped["b", k], WARM[1])
             if k == 0:
                 gather(0, 2)
-            copy_chunk_vector("b", k, VECTOR_T[k])
+            copy_chunk_vector(m2, k, VECTOR_T[k])
             if k == 1 and not X0_SOON:
                 quantise_x(0)
             if not (SPLIT_LAST and k == STAGES - 1):
-                quantise_chunk("b", k)
+                quantise_chunk(m2, k)
             if k == 0:
                 gather(1, 2)
             if k == 1:
@@ -502,8 +555,8 @@ def tile_routed_moe_kernel(tc, xT, w1, w3, w2, gate, offs, out):
             if k >= 1:
                 first_layer(k)
             if k + AHEAD < STAGES:
-                load_chunk("a", k + AHEAD)
-                load_chunk("b", k + AHEAD)
+                for m in order_of(k + AHEAD):
+                    load_chunk(m, k + AHEAD)
                 if LOADS3 and k in W_AT:
                     for f in W_AT[k]:
                         load_w2(f)
@@ -520,13 +573,18 @@ def tile_routed_moe_kernel(tc, xT, w1, w3, w2, gate, offs, out):
                 quantise_w2(e)
             if k >= 2 and not (HOLD_SC and k == STAGES - 1):
                 scatter((k - 2) // 2, 0, 2, hc)
+            if HOLD_HALF and k == STAGES - 1:
+                scatter_held(0)
             if k == 1:
                 hidden_values(0)
             if k >= 1:
                 hidden_values(k)
             if HOLD_SC and k == STAGES - 1:
                 copy_held_y()
-                scatter(E - 2, 0, 2, 1)
+                if HOLD_HALF:
+                    scatter_held(1)
+                else:
+                    scatter(E - 2, 0, 2, 1)
             if hc == 1 and e + 1 < E:
                 second_layer(e, 0, 2)
             if hc == 0 and k >= 2 and not (W2_LAST_ON_S and e == E - 1):

@@ -37,12 +37,14 @@ ONE_RING = False
 ALIAS_G1 = False
 PLANES_FIRST = False
 G1_AT = 0
+HEAD = ("p0", "a0", "p1", "b0", "p2", "a1", "p3", "b1")
 PB4 = True
 WARM_FROM = 0
 WARM = ()
 F_GROUPS = ()
 SPLIT_LAST = False
 X_V_EXPERTS = (0, 1, 2, 3)
+HOLD_MID = True
 HOLD_HALF = True
 HOLD_SC = True
 WIDE_G = 1376
@@ -329,7 +331,9 @@ def tile_routed_moe_kernel(tc, xT, w1, w3, w2, gate, offs, out):
                 hidden[e] = hid.tile([P, 2, 2, HALF, 4], BF16, name="hg", align_bytes=64)
             last = TAIL_G and e == E - 1
             for s in range(2):
-                if HOLD_SC and u == STAGES - 1 and s == 1:
+                if HOLD_MID and u in (3, 5) and s == 1:
+                    gelus[u, s] = alias.tile([P, HALF, 4], F32, name="held%d" % u)
+                elif HOLD_SC and u == STAGES - 1 and s == 1:
                     gelus[u, s] = alias.tile([P, HALF, 4], F32, name="held")
                 else:
                     gelus[u, s] = gel.tile([P, HALF, 4], F32, name="ga")
@@ -348,6 +352,7 @@ def tile_routed_moe_kernel(tc, xT, w1, w3, w2, gate, offs, out):
 
         tail_sums = {}
         held_y = {}
+        mid_y = {}
 
         def tail_pass(g):
             e = E - 1
@@ -397,6 +402,10 @@ def tile_routed_moe_kernel(tc, xT, w1, w3, w2, gate, offs, out):
                         )
 
         def copy_y(e, lo, hi):
+            if HOLD_MID and e < E - 2:
+                mid_y[e, 0] = hid.tile([P, 2, HALF], F32, name="y")
+                nc.scalar.copy(out=mid_y[e, 0][:], in_=sums[e, lo][:, :, 0, :])
+                return
             if HOLD_SC and e == E - 2:
                 if HOLD_HALF:
                     held_y[0] = hid.tile([P, 3, HALF], F32, name="y")
@@ -408,6 +417,10 @@ def tile_routed_moe_kernel(tc, xT, w1, w3, w2, gate, offs, out):
                 return
             ys[e, lo] = hid.tile([P, 2, hi - lo, HALF], F32, name="y")
             nc.scalar.copy(out=ys[e, lo][:], in_=sums[e, lo][:].rearrange("p s b n -> p b s n"))
+
+        def copy_mid_y(e):
+            mid_y[e, 1] = alias.tile([P, 2, HALF], F32, name="held%d" % (2 * e + 3))
+            nc.scalar.copy(out=mid_y[e, 1][:], in_=sums[e, 0][:, :, 1, :])
 
         def copy_held_y():
             if HOLD_HALF:
@@ -432,7 +445,11 @@ def tile_routed_moe_kernel(tc, xT, w1, w3, w2, gate, offs, out):
             nc.vector.tensor_tensor(
                 out=windows[nb][:].indirect(offsets[:, first // 16 : last // 16]),
                 in0=(
-                    (held_y[0][:, 0:2, :] if HOLD_HALF else held_y[nb][:]) if HOLD_SC and e == E - 2 else ys[e, lo][:, nb, :, :]
+                    mid_y[e, nb][:]
+                    if HOLD_MID and e < E - 2
+                    else (held_y[0][:, 0:2, :] if HOLD_HALF else held_y[nb][:])
+                    if HOLD_SC and e == E - 2
+                    else ys[e, lo][:, nb, :, :]
                 ).rearrange("p s n -> p (s n)"),
                 in1=gate_of(e, nb, lo, hi),
                 op=MULT,
@@ -441,10 +458,12 @@ def tile_routed_moe_kernel(tc, xT, w1, w3, w2, gate, offs, out):
         if PLANES_FIRST:
             for c in range(4):
                 load_plane(c)
-        for c in range(4):
-            if not PLANES_FIRST:
-                load_plane(c)
-            load_chunk(order_of(c // 2)[c % 2], c // 2)
+        for item in HEAD:
+            if item[0] == "p":
+                if not PLANES_FIRST:
+                    load_plane(int(item[1]))
+            else:
+                load_chunk(item[0], int(item[1]))
         if LOADS3:
             for m in order_of(2):
                 load_chunk(m, 2)
@@ -571,7 +590,7 @@ def tile_routed_moe_kernel(tc, xT, w1, w3, w2, gate, offs, out):
                 copy_w2(0)
             if hc == 1 and not (W2_LAST_ON_S and e == E - 1):
                 quantise_w2(e)
-            if k >= 2 and not (HOLD_SC and k == STAGES - 1):
+            if k >= 2 and not (HOLD_SC and k == STAGES - 1) and not (HOLD_MID and k in (3, 5)):
                 scatter((k - 2) // 2, 0, 2, hc)
             if HOLD_HALF and k == STAGES - 1:
                 scatter_held(0)
@@ -579,6 +598,9 @@ def tile_routed_moe_kernel(tc, xT, w1, w3, w2, gate, offs, out):
                 hidden_values(0)
             if k >= 1:
                 hidden_values(k)
+            if HOLD_MID and k in (3, 5):
+                copy_mid_y((k - 3) // 2)
+                scatter((k - 3) // 2, 0, 2, 1)
             if HOLD_SC and k == STAGES - 1:
                 copy_held_y()
                 if HOLD_HALF:

@@ -38,12 +38,13 @@ ALIAS_G1 = False
 PLANES_FIRST = False
 G1_AT = 0
 HEAD = ("p0", "a0", "p1", "b0", "p2", "a1", "p3", "b1")
-PB4 = True
-WARM_FROM = 0
+PB4 = False
+WARM_FROM = 1
 WARM = ()
 F_GROUPS = ()
 SPLIT_LAST = False
 X_V_EXPERTS = (0, 1, 2, 3)
+Y_ON_V = False
 HOLD_MID = True
 HOLD_HALF = True
 HOLD_SC = True
@@ -401,16 +402,18 @@ def tile_routed_moe_kernel(tc, xT, w1, w3, w2, gate, offs, out):
                             stop=(g == 1),
                         )
 
+        y_copy = nc.vector.tensor_copy if Y_ON_V else nc.scalar.copy
+
         def copy_y(e, lo, hi):
             if HOLD_MID and e < E - 2:
                 mid_y[e, 0] = hid.tile([P, 2, HALF], F32, name="y")
-                nc.scalar.copy(out=mid_y[e, 0][:], in_=sums[e, lo][:, :, 0, :])
+                y_copy(out=mid_y[e, 0][:], in_=sums[e, lo][:, :, 0, :])
                 return
             if HOLD_SC and e == E - 2:
                 if HOLD_HALF:
                     held_y[0] = hid.tile([P, 3, HALF], F32, name="y")
-                    nc.scalar.copy(out=held_y[0][:, 0:2, :], in_=sums[e, lo][:, :, 0, :])
-                    nc.scalar.copy(out=held_y[0][:, 2, :], in_=sums[e, lo][:, 0, 1, :])
+                    y_copy(out=held_y[0][:, 0:2, :], in_=sums[e, lo][:, :, 0, :])
+                    y_copy(out=held_y[0][:, 2, :], in_=sums[e, lo][:, 0, 1, :])
                     return
                 held_y[0] = hid.tile([P, 2, HALF], F32, name="y")
                 nc.scalar.copy(out=held_y[0][:], in_=sums[e, lo][:, :, 0, :])
@@ -420,12 +423,12 @@ def tile_routed_moe_kernel(tc, xT, w1, w3, w2, gate, offs, out):
 
         def copy_mid_y(e):
             mid_y[e, 1] = alias.tile([P, 2, HALF], F32, name="held%d" % (2 * e + 3))
-            nc.scalar.copy(out=mid_y[e, 1][:], in_=sums[e, 0][:, :, 1, :])
+            y_copy(out=mid_y[e, 1][:], in_=sums[e, 0][:, :, 1, :])
 
         def copy_held_y():
             if HOLD_HALF:
                 held_y[1] = alias.tile([P, HALF], F32, name="held")
-                nc.scalar.copy(out=held_y[1][:], in_=sums[E - 2, 0][:, 1, 1, :])
+                y_copy(out=held_y[1][:], in_=sums[E - 2, 0][:, 1, 1, :])
                 return
             held_y[1] = alias.tile([P, 2, HALF], F32, name="held")
             nc.scalar.copy(out=held_y[1][:], in_=sums[E - 2, 0][:, :, 1, :])

from contextlib import ExitStack

import concourse.mybir as mybir

K, T, E, C, H, N = 512, 1024, 4, 256, 1024, 256
FLOPS = 2 * E * C * (2 * K * H + H * N)

F32 = mybir.dt.float32
BF16 = mybir.dt.bfloat16
U32 = mybir.dt.uint32
U16 = mybir.dt.uint16
U8 = mybir.dt.uint8
FP8X4 = mybir.dt.float8_e4m3fn_x4
GELU = mybir.ActivationFunctionType.Gelu_apprx_tanh
COPY = mybir.ActivationFunctionType.Copy
MULT = mybir.AluOpType.mult
ADD = mybir.AluOpType.add

P = 128
HC = 512
HALF = 128
GROUP = 512
STAGES = 2 * E
AHEAD = 4
VECTOR_T = (0, 0, 0, 0, 0, 0, 0, 0)
MERGE_W2 = True
W2_ON_S = ()
X0_SOON = False
W2_LAST_ON_S = False
TAIL_G = False
TAIL_NB = False
CUT = 0
W0_LATE = False
W_AT = {0: (1,), 2: (2,), 3: (3,)}
LOADS3 = True
ONE_RING = False
ALIAS_G1 = False
PLANES_FIRST = False
G1_AT = 0
HEAD = ("p0", "a0", "p1", "b0", "p2", "a1", "p3", "b1")
PB4 = False
WARM_FROM = 1
WARM = ()
F_GROUPS = ()
SPLIT_LAST = False
X_V_EXPERTS = (0, 1, 2, 3)
Y_ON_V = False
HOLD_MID = True
HOLD_HALF = True
HOLD_SC = True
WIDE_G = 1376
B_FIRST = False
X_PAIRS = False
X_ON_V = True
X_EARLY = False
GPS_X = False
MERGE_X1 = False


def tile_routed_moe_kernel(tc, xT, w1, w3, w2, gate, offs, out):
    nc = tc.nc
    with ExitStack() as ctx:
        lists = ctx.enter_context(tc.tile_pool(name="lists", bufs=1))
        keep = ctx.enter_context(tc.tile_pool(name="keep", bufs=1))
        rawc = ctx.enter_context(tc.tile_pool(name="rawc", bufs=2 * AHEAD + 3 if ONE_RING else 2 * AHEAD))
        raw2 = ctx.enter_context(tc.tile_pool(name="raw2", bufs=3))
        stage13 = ctx.enter_context(tc.tile_pool(name="stage13", bufs=4))
        stage2 = ctx.enter_context(tc.tile_pool(name="stage2", bufs=2))
        wq = ctx.enter_context(tc.tile_pool(name="wq", bufs=3))
        hid = ctx.enter_context(tc.tile_pool(name="hid", bufs=2))
        gel = ctx.enter_context(tc.tile_pool(name="gel", bufs=4))
        psum_ab = ctx.enter_context(tc.psum_pool(name="psum_ab", bufs=4 if PB4 else 3))
        psum_a2 = ctx.enter_context(tc.psum_pool(name="psum_a2", bufs=2)) if WARM or WARM_FROM or PB4 else psum_ab
        psum_w = ctx.enter_context(tc.psum_pool(name="psum_w", bufs=1)) if WARM or WARM_FROM else psum_ab
        psum_y = ctx.enter_context(tc.psum_pool(name="psum_y", bufs=2))

        offsets = lists.tile([P, T // 16], U16, name="offsets")
        nc.sync.dma_start(offsets[:], offs)

        warm = keep.tile([P, 1], F32, name="warm")
        warmed = keep.tile([P, 1], F32, name="warmed")
        nc.gpsimd.memset(warm[:], 0.0)
        nc.scalar.activation(out=warmed[:], in_=warm[:], func=GELU)

        x_rows = xT.rearrange("(p t) n -> p t n", t=4)
        planes = [keep.tile([P, WIDE_G or T], F32, name="plane%d" % t) for t in range(4)]
        if LOADS3:
            gates = [keep.tile([P, 2, C], F32, name="gate%d" % e) for e in range(E)]
        else:
            gates = [keep.tile([P, E * C], F32, name="gate%d" % nb) for nb in range(2)]
        windows = [keep.tile([P, T], F32, name="window%d" % nb) for nb in range(2)]
        if WIDE_G:
            gathered = [keep.tile([P, 4, E * C], F32, name="g4")]
        else:
            gathered = [keep.tile([P, 4, GROUP], F32, name="g4_%d" % gi) for gi in range(1 if ALIAS_G1 else E * C // GROUP)]
        alias = ctx.enter_context(tc.tile_pool(name="alias", bufs=1))
        pairs = {}
        sources = {"a": w1, "b": w3}
        raw, grouped, codes, scales = {}, {}, {}, {}
        raw_w2, grouped_w2, q_w2 = {}, {}, {}
        xg, x_codes, x_scales, x_col0 = {}, {}, {}, {}
        banks, gelus, hidden, sums, ys = {}, {}, {}, {}, {}

        def order_of(u):
            return ("b", "a") if B_FIRST and u < STAGES - 1 else ("a", "b")

        def load_plane(t):
            nc.sync.dma_start(out=planes[t][:, 0:T], in_=x_rows[:, t, :])

        def load_gates():
            for nb in range(2):
                nc.sync.dma_start(out=gates[nb][:], in_=gate[P * nb : P * (nb + 1), :])

        def load_gate(e):
            nc.sync.dma_start(out=gates[e][:], in_=gate.rearrange("(b p) n -> p b n", b=2)[:, :, C * e : C * (e + 1)])

        def gate_of(e, nb, lo, hi):
            if LOADS3:
                return gates[e][:, nb, HALF * lo : HALF * hi]
            return gates[nb][:, C * e + HALF * lo : C * e + HALF * hi]

        def load_chunk(m, u):
            raw[m, u] = rawc.tile([P, 4, HC], F32, name="rawc")
            cols = slice(HC * (u % 2), HC * (u % 2 + 1))
            nc.sync.dma_start(
                out=raw[m, u][:], in_=sources[m][u // 2, :, :].rearrange("(p j) c -> p j c", j=4)[:, :, cols]
            )

        def load_w2(e):
            raw_w2[e] = rawc.tile([P, 2, 4, N], F32, name="rawc") if ONE_RING else raw2.tile([P, 2, 4, N], F32, name="raw2")
            nc.sync.dma_start(out=raw_w2[e][:], in_=w2[e, :, :].rearrange("(g p j) n -> p g j n", g=2, j=4))

        planes16 = {}

        def gather(gi, t):
            if WIDE_G:
                if gi == 0:
                    nc.vector.tensor_copy(out=gathered[0][:, t, :], in_=planes[t][:].indirect(offsets[:]))
                return
            if gi in F_GROUPS and t < 2:
                if t not in planes16:
                    planes16[t] = keep.tile([P, T], BF16, name="plane16_%d" % t)
                    nc.scalar.copy(out=planes16[t][:], in_=planes[t][:])
                for e in (2 * gi, 2 * gi + 1):
                    if e not in xg:
                        xg[e] = keep.tile([P, C, 4], BF16, name="xg%d" % e, align_bytes=64)
                    nc.scalar.activation(
                        out=xg[e][:, :, t],
                        in_=planes16[t][:].indirect(offsets[:, C * e // 16 : C * (e + 1) // 16]),
                        func=COPY,
                    )
                return
            if ALIAS_G1 and gi == 1:
                if t % 2 == 0:
                    pairs[t // 2] = alias.tile([P, 2, GROUP], F32, name="al%d" % (t // 2), align_bytes=64)
                nc.vector.tensor_copy(
                    out=pairs[t // 2][:, t % 2, :],
                    in_=planes[t][:].indirect(offsets[:, GROUP * gi // 16 : GROUP * (gi + 1) // 16]),
                )
                return
            nc.vector.tensor_copy(
                out=gathered[gi][:, t, :],
                in_=planes[t][:].indirect(offsets[:, GROUP * gi // 16 : GROUP * (gi + 1) // 16]),
            )

        def copy_x(e):
            if X_PAIRS:
                if e % 2 == 0:
                    xg[e] = keep.tile([P, GROUP, 4], BF16, name="xgp%d" % e, align_bytes=64)
                    nc.vector.tensor_copy(
                        out=xg[e][:].rearrange("p (c i) t -> p c t i", i=4),
                        in_=gathered[e // 2][:].rearrange("p t (c i) -> p c t i", i=4),
                    )
                return
            if MERGE_X1 and e >= 2:
                if e == 2:
                    xg[2] = keep.tile([P, GROUP, 4], BF16, name="xg23", align_bytes=64)
                    nc.scalar.copy(
                        out=xg[2][:].rearrange("p (c i) t -> p c t i", i=4),
                        in_=gathered[1][:].rearrange("p t (c i) -> p c t i", i=4),
                    )
                return
            col0 = e * C % GROUP
            if e // 2 in F_GROUPS:
                nc.vector.tensor_copy(
                    out=xg[e][:].rearrange("p (c i) t -> p c t i", i=4)[:, :, 2:4, :],
                    in_=gathered[e // 2][:, 2:4, col0 : col0 + C].rearrange("p t (c i) -> p c t i", i=4),
                )
                return
            xg[e] = keep.tile([P, C, 4], BF16, name="xg%d" % e, align_bytes=64)
            if ALIAS_G1 and e >= 2:
                for h in range(2):
                    nc.vector.tensor_copy(
                        out=xg[e][:].rearrange("p (c i) t -> p c t i", i=4)[:, :, 2 * h : 2 * h + 2, :],
                        in_=pairs[h][:, :, col0 : col0 + C].rearrange("p t (c i) -> p c t i", i=4),
                    )
                return
            if GPS_X:
                nc.gpsimd.tensor_scalar(
                    out=xg[e][:],
                    in0=gathered[e * C // GROUP][:, :, col0 : col0 + C].rearrange("p t c -> p c t"),
                    scalar1=1.0,
                    scalar2=0.0,
                    op0=MULT,
                    op1=ADD,
                )
                return
            (nc.vector.tensor_copy if X_ON_V and e in X_V_EXPERTS else nc.scalar.copy)(
                out=xg[e][:].rearrange("p (c i) t -> p c t i", i=4),
                in_=(
                    gathered[0][:, :, C * e : C * (e + 1)] if WIDE_G else gathered[e * C // GROUP][:, :, col0 : col0 + C]
                ).rearrange("p t (c i) -> p c t i", i=4),
            )

        def quantise_x(e):
            if X_PAIRS:
                if e % 2 == 0:
                    xc = keep.tile([P, GROUP], U32, name="xcp%d" % e, align_bytes=64)
                    xs = keep.tile([P, GROUP], U8, name="xsp%d" % e, align_bytes=64)
                    nc.vector.quantize_mx(
                        out=xc[:].bitcast(FP8X4), scales=xs[:], in_=xg[e][:].rearrange("p n t -> p (n t)")
                    )
                    for f in (e, e + 1):
                        x_codes[f], x_scales[f], x_col0[f] = xc, xs, C * (f - e)
                return
            if MERGE_X1 and e >= 2:
                if e == 2:
                    xc = keep.tile([P, GROUP], U32, name="xc23", align_bytes=64)
                    xs = keep.tile([P, GROUP], U8, name="xs23", align_bytes=64)
                    nc.vector.quantize_mx(
                        out=xc[:].bitcast(FP8X4), scales=xs[:], in_=xg[2][:].rearrange("p n t -> p (n t)")
                    )
                    for f in (2, 3):
                        x_codes[f], x_scales[f], x_col0[f] = xc, xs, C * (f - 2)
                return
            x_codes[e] = keep.tile([P, C], U32, name="xc%d" % e, align_bytes=64)
            x_scales[e] = keep.tile([P, C], U8, name="xs%d" % e, align_bytes=64)
            x_col0[e] = 0
            nc.vector.quantize_mx(
                out=x_codes[e][:].bitcast(FP8X4), scales=x_scales[e][:], in_=xg[e][:].rearrange("p n t -> p (n t)")
            )

        def views(m, u, t0, t1):
            dst = grouped[m, u][:, HC * t0 : HC * t1].rearrange("p (t i j) -> p i j t", t=t1 - t0, j=4)
            src = raw[m, u][:].rearrange("p j (i t) -> p i j t", t=4)[:, :, :, t0:t1]
            return dst, src

        def split_chunk(m, u):
            grouped[m, u] = stage13.tile([P, 4 * HC], BF16, name="grouped13", align_bytes=64)
            codes[m, u] = wq.tile([P, HC], U32, name="c" + m, align_bytes=64)
            scales[m, u] = wq.tile([P, HC], U8, name="s" + m, align_bytes=64)
            for half in range(2):
                dst, src = views(m, u, 2 * half, 2 * half + 2)
                nc.scalar.copy(out=dst, in_=src)
                nc.vector.quantize_mx(
                    out=codes[m, u][:, 2 * P * half : 2 * P * (half + 1)].bitcast(FP8X4),
                    scales=scales[m, u][:, 2 * P * half : 2 * P * (half + 1)],
                    in_=grouped[m, u][:, 2 * HC * half : 2 * HC * (half + 1)],
                )

        def copy_chunk_scalar(m, u, vector_t):
            if ALIAS_G1 and u == 0:
                grouped[m, u] = alias.tile([P, 4 * HC], BF16, name="al%d" % "ab".index(m), align_bytes=64)
            else:
                grouped[m, u] = stage13.tile([P, 4 * HC], BF16, name="grouped13", align_bytes=64)
            dst, src = views(m, u, 0, 4 - vector_t)
            nc.scalar.copy(out=dst, in_=src)
            if WARM_FROM and u >= WARM_FROM:
                keep_warm(grouped[m, u], 1)

        def copy_chunk_vector(m, u, vector_t):
            if vector_t > 0:
                dst, src = views(m, u, 4 - vector_t, 4)
                nc.vector.tensor_copy(out=dst, in_=src)

        def quantise_chunk(m, u):
            codes[m, u] = wq.tile([P, HC], U32, name="c" + m, align_bytes=64)
            scales[m, u] = wq.tile([P, HC], U8, name="s" + m, align_bytes=64)
            nc.vector.quantize_mx(out=codes[m, u][:].bitcast(FP8X4), scales=scales[m, u][:], in_=grouped[m, u][:])

        def copy_w2(e):
            grouped_w2[e] = stage2.tile([P, 2, N, 4], BF16, name="grouped2", align_bytes=64)
            on_scalar = (W2_LAST_ON_S and e == E - 1) or e in W2_ON_S
            if MERGE_W2 and not on_scalar:
                nc.vector.tensor_copy(
                    out=grouped_w2[e][:].rearrange("p g (c i) j -> p g c j i", i=4),
                    in_=raw_w2[e][:].rearrange("p g j (c i) -> p g c j i", i=4),
                )
                return
            for g in range(2):
                (nc.scalar.copy if on_scalar else nc.vector.tensor_copy)(
                    out=grouped_w2[e][:, g, :, :].rearrange("p (c i) j -> p c j i", i=4),
                    in_=raw_w2[e][:, g, :, :].rearrange("p j (c i) -> p c j i", i=4),
                )

        def quantise_w2(e):
            c2 = wq.tile([P, 2, N], U32, name="cw2", align_bytes=64)
            s2 = wq.tile([P, 2, N], U8, name="sw2", align_bytes=64)
            nc.vector.quantize_mx(
                out=c2[:].rearrange("p g n -> p (g n)").bitcast(FP8X4),
                scales=s2[:].rearrange("p g n -> p (g n)"),
                in_=grouped_w2[e][:].rearrange("p g n j -> p (g n j)"),
            )
            q_w2[e] = (c2, s2)

        def keep_warm(source, count):
            for j in range(count):
                idle_bank = psum_w.tile([P, 512], F32, name="pw")
                nc.tensor.matmul(idle_bank[:], lhsT=source[:, 0:P], rhs=source[:, 512 * j : 512 * (j + 1)], start=True, stop=True)

        def first_layer(u):
            e = u // 2
            for m in order_of(u):
                split = SPLIT_LAST and m == "b" and u == STAGES - 1
                for s, ts in ((0, (0, 1)), (1, (0, 1)), (0, (2, 3)), (1, (2, 3))) if split else ((0, range(4)), (1, range(4))):
                    if ts[0] == 0:
                        banks[m, u, s] = (psum_a2 if (WARM or WARM_FROM or PB4) and m == "a" else psum_ab).tile([P, 4, HALF], F32, name="p" + m)
                    for t in ts:
                        nc.tensor.matmul_mx(
                            out=banks[m, u, s][:, t, :],
                            lhsT=codes[m, u][:, P * t : P * (t + 1)].bitcast(FP8X4),
                            lhsT_scale=scales[m, u][:, P * t : P * (t + 1)],
                            rhs=x_codes[e][:, x_col0[e] + HALF * s : x_col0[e] + HALF * (s + 1)].bitcast(FP8X4),
                            rhs_scale=x_scales[e][:, x_col0[e] + HALF * s : x_col0[e] + HALF * (s + 1)],
                            start=True,
                            stop=True,
                        )

        def hidden_values(u):
            e, hc = u // 2, u % 2
            if hc == 0:
                hidden[e] = hid.tile([P, 2, 2, HALF, 4], BF16, name="hg", align_bytes=64)
            last = TAIL_G and e == E - 1
            for s in range(2):
                if HOLD_MID and u in (3, 5) and s == 1:
                    gelus[u, s] = alias.tile([P, HALF, 4], F32, name="held%d" % u)
                elif HOLD_SC and u == STAGES - 1 and s == 1:
                    gelus[u, s] = alias.tile([P, HALF, 4], F32, name="held")
                else:
                    gelus[u, s] = gel.tile([P, HALF, 4], F32, name="ga")
                nc.scalar.activation(out=gelus[u, s][:], in_=banks["a", u, s][:].rearrange("p t n -> p n t"), func=GELU)
            if W2_LAST_ON_S and u == STAGES - 1:
                copy_w2(E - 1)
            for s in range(2):
                nc.vector.tensor_tensor(
                    out=hidden[e][:, hc, s, :, :] if last else hidden[e][:, s, hc, :, :],
                    in0=banks["b", u, s][:].rearrange("p t n -> p n t"),
                    in1=gelus[u, s][:],
                    op=MULT,
                )
                if WARM and u == STAGES - 1:
                    keep_warm(hidden[e][:, s, :, :, :].rearrange("p g n t -> p (g n t)"), WARM[2])

        tail_sums = {}
        held_y = {}
        mid_y = {}

        def tail_pass(g):
            e = E - 1
            t_codes = hid.tile([P, C], U32, name="tcodes", align_bytes=64)
            t_scales = hid.tile([P, C], U8, name="tscales", align_bytes=64)
            nc.vector.quantize_mx(
                out=t_codes[:].bitcast(FP8X4),
                scales=t_scales[:],
                in_=hidden[e][:, g, :, :, :].rearrange("p s n t -> p (s n t)"),
            )
            c2, s2 = q_w2[e]
            for nb in range(2):
                if g == 0:
                    tail_sums[nb] = psum_y.tile([P, C], F32, name="py")
                nc.tensor.matmul_mx(
                    out=tail_sums[nb][:],
                    lhsT=c2[:, g, P * nb : P * (nb + 1)].bitcast(FP8X4),
                    lhsT_scale=s2[:, g, P * nb : P * (nb + 1)],
                    rhs=t_codes[:].bitcast(FP8X4),
                    rhs_scale=t_scales[:],
                    start=(g == 0),
                    stop=(g == 1),
                )

        def second_layer(e, lo, hi):
            parts = hi - lo
            h_codes = hid.tile([P, parts, 2, HALF], U32, name="hcodes", align_bytes=64)
            h_scales = hid.tile([P, parts, 2, HALF], U8, name="hscales", align_bytes=64)
            nc.vector.quantize_mx(
                out=h_codes[:].rearrange("p s g n -> p (s g n)").bitcast(FP8X4),
                scales=h_scales[:].rearrange("p s g n -> p (s g n)"),
                in_=hidden[e][:, lo:hi, :, :, :].rearrange("p s g n t -> p (s g n t)"),
            )
            c2, s2 = q_w2[e]
            sums[e, lo] = psum_y.tile([P, parts, 2, HALF], F32, name="py")
            for s in range(parts):
                for nb in range(2):
                    for g in range(2):
                        nc.tensor.matmul_mx(
                            out=sums[e, lo][:, s, nb, :],
                            lhsT=c2[:, g, P * nb : P * (nb + 1)].bitcast(FP8X4),
                            lhsT_scale=s2[:, g, P * nb : P * (nb + 1)],
                            rhs=h_codes[:, s, g, :].bitcast(FP8X4),
                            rhs_scale=h_scales[:, s, g, :],
                            start=(g == 0),
                            stop=(g == 1),
                        )

        y_copy = nc.vector.tensor_copy if Y_ON_V else nc.scalar.copy

        def copy_y(e, lo, hi):
            if HOLD_MID and e < E - 2:
                mid_y[e, 0] = hid.tile([P, 2, HALF], F32, name="y")
                y_copy(out=mid_y[e, 0][:], in_=sums[e, lo][:, :, 0, :])
                return
            if HOLD_SC and e == E - 2:
                if HOLD_HALF:
                    held_y[0] = hid.tile([P, 3, HALF], F32, name="y")
                    y_copy(out=held_y[0][:, 0:2, :], in_=sums[e, lo][:, :, 0, :])
                    y_copy(out=held_y[0][:, 2, :], in_=sums[e, lo][:, 0, 1, :])
                    return
                held_y[0] = hid.tile([P, 2, HALF], F32, name="y")
                nc.scalar.copy(out=held_y[0][:], in_=sums[e, lo][:, :, 0, :])
                return
            ys[e, lo] = hid.tile([P, 2, hi - lo, HALF], F32, name="y")
            nc.scalar.copy(out=ys[e, lo][:], in_=sums[e, lo][:].rearrange("p s b n -> p b s n"))

        def copy_mid_y(e):
            mid_y[e, 1] = alias.tile([P, 2, HALF], F32, name="held%d" % (2 * e + 3))
            y_copy(out=mid_y[e, 1][:], in_=sums[e, 0][:, :, 1, :])

        def copy_held_y():
            if HOLD_HALF:
                held_y[1] = alias.tile([P, HALF], F32, name="held")
                y_copy(out=held_y[1][:], in_=sums[E - 2, 0][:, 1, 1, :])
                return
            held_y[1] = alias.tile([P, 2, HALF], F32, name="held")
            nc.scalar.copy(out=held_y[1][:], in_=sums[E - 2, 0][:, :, 1, :])

        def scatter_held(part):
            e = E - 2
            first = C * e + HALF * part
            nc.vector.tensor_tensor(
                out=windows[1][:].indirect(offsets[:, first // 16 : (first + HALF) // 16]),
                in0=held_y[0][:, 2, :] if part == 0 else held_y[1][:],
                in1=gate_of(e, 1, part, part + 1),
                op=MULT,
            )

        def scatter(e, lo, hi, nb):
            first, last = C * e + HALF * lo, C * e + HALF * hi
            nc.vector.tensor_tensor(
                out=windows[nb][:].indirect(offsets[:, first // 16 : last // 16]),
                in0=(
                    mid_y[e, nb][:]
                    if HOLD_MID and e < E - 2
                    else (held_y[0][:, 0:2, :] if HOLD_HALF else held_y[nb][:])
                    if HOLD_SC and e == E - 2
                    else ys[e, lo][:, nb, :, :]
                ).rearrange("p s n -> p (s n)"),
                in1=gate_of(e, nb, lo, hi),
                op=MULT,
            )

        if PLANES_FIRST:
            for c in range(4):
                load_plane(c)
        for item in HEAD:
            if item[0] == "p":
                if not PLANES_FIRST:
                    load_plane(int(item[1]))
            else:
                load_chunk(item[0], int(item[1]))
        if LOADS3:
            for m in order_of(2):
                load_chunk(m, 2)
            if not W0_LATE:
                load_w2(0)
                load_gate(0)
            for m in order_of(3):
                load_chunk(m, 3)
            if W0_LATE:
                load_w2(0)
                load_gate(0)
        else:
            load_w2(0)
            load_chunk("a", 2)
            load_chunk("b", 2)
            load_gates()
            load_chunk("a", 3)
            load_chunk("b", 3)
            load_w2(1)

        if PLANES_FIRST:
            for t in range(4):
                gather(0, t)
            copy_x(0)
            quantise_x(0)
        else:
            gather(0, 0)
            gather(1, 0)
        if CUT:
            for nb in range(2):
                nc.gpsimd.memset(windows[nb][:], 0.0)
        for k in range(STAGES if PLANES_FIRST else 0):
            e, hc = k // 2, k % 2
            copy_chunk_scalar("a", k, 0)
            quantise_chunk("a", k)
            copy_chunk_scalar("b", k, VECTOR_T[k])
            copy_chunk_vector("b", k, VECTOR_T[k])
            quantise_chunk("b", k)
            first_layer(k)
            if k + AHEAD < STAGES:
                load_chunk("a", k + AHEAD)
                load_chunk("b", k + AHEAD)
                if LOADS3 and k in W_AT:
                    for f in W_AT[k]:
                        load_w2(f)
                        load_gate(f)
                if hc == 1 and not LOADS3:
                    load_w2((k + AHEAD) // 2)
            if k >= 2 and hc == 0:
                copy_y(e - 1, 0, 2)
            if hc == 1 and e + 1 < E:
                copy_x(e + 1)
            if hc == 1 and not (W2_LAST_ON_S and e == E - 1):
                quantise_w2(e)
            if k >= 2 and not (HOLD_SC and k == STAGES - 1):
                scatter((k - 2) // 2, 0, 2, hc)
            if HOLD_HALF and k == STAGES - 1:
                scatter_held(0)
            hidden_values(k)
            if HOLD_SC and k == STAGES - 1:
                copy_held_y()
                if HOLD_HALF:
                    scatter_held(1)
                else:
                    scatter(E - 2, 0, 2, 1)
            if hc == 1 and e + 1 < E:
                second_layer(e, 0, 2)
            if hc == 0 and not (W2_LAST_ON_S and e == E - 1):
                copy_w2(e)
            if hc == 1 and e + 1 < E:
                quantise_x(e + 1)
            if k == G1_AT:
                for t in range(4):
                    gather(1, t)
        for k in range(0 if PLANES_FIRST else (CUT or STAGES)):
            e, hc = k // 2, k % 2
            m1, m2 = order_of(k)
            copy_chunk_scalar(m1, k, 0)
            if WARM and k == STAGES - 1:
                keep_warm(grouped["a", k], WARM[0])
            if k < 2:
                gather(0, 2 * k + 1)
            if k == 1 and X0_SOON:
                copy_x(0)
                quantise_x(0)
            quantise_chunk(m1, k)
            if k < 2:
                gather(1, 2 * k + 1)
            if k == 1 and not X0_SOON:
                copy_x(0)
            if SPLIT_LAST and k == STAGES - 1:
                split_chunk("b", k)
            else:
                copy_chunk_scalar(m2, k, VECTOR_T[k])
            if WARM and k == STAGES - 1:
                keep_warm(grouped["b", k], WARM[1])
            if k == 0:
                gather(0, 2)
            copy_chunk_vector(m2, k, VECTOR_T[k])
            if k == 1 and not X0_SOON:
                quantise_x(0)
            if not (SPLIT_LAST and k == STAGES - 1):
                quantise_chunk(m2, k)
            if k == 0:
                gather(1, 2)
            if k == 1:
                first_layer(0)
            if k >= 1:
                first_layer(k)
            if k + AHEAD < STAGES:
                for m in order_of(k + AHEAD):
                    load_chunk(m, k + AHEAD)
                if LOADS3 and k in W_AT:
                    for f in W_AT[k]:
                        load_w2(f)
                        load_gate(f)
                if hc == 1 and not LOADS3:
                    load_w2((k + AHEAD) // 2)
            if k >= 2 and hc == 0:
                copy_y(e - 1, 0, 2)
            if hc == 1 and e + 1 < E and not (X_EARLY and e >= 1):
                copy_x(e + 1)
            if k == 1:
                copy_w2(0)
            if hc == 1 and not (W2_LAST_ON_S and e == E - 1):
                quantise_w2(e)
            if k >= 2 and not (HOLD_SC and k == STAGES - 1) and not (HOLD_MID and k in (3, 5)):
                scatter((k - 2) // 2, 0, 2, hc)
            if HOLD_HALF and k == STAGES - 1:
                scatter_held(0)
            if k == 1:
                hidden_values(0)
            if k >= 1:
                hidden_values(k)
            if HOLD_MID and k in (3, 5):
                copy_mid_y((k - 3) // 2)
                scatter((k - 3) // 2, 0, 2, 1)
            if HOLD_SC and k == STAGES - 1:
                copy_held_y()
                if HOLD_HALF:
                    scatter_held(1)
                else:
                    scatter(E - 2, 0, 2, 1)
            if hc == 1 and e + 1 < E:
                second_layer(e, 0, 2)
            if hc == 0 and k >= 2 and not (W2_LAST_ON_S and e == E - 1):
                copy_w2(e)
            if hc == 1 and e + 1 < E:
                quantise_x(e + 1)
            if X_EARLY and k == 1:
                copy_x(2)
                copy_x(3)
        if W2_LAST_ON_S:
            quantise_w2(E - 1)
        if CUT:
            for nb in range(2):
                nc.sync.dma_start(out=out[P * nb : P * (nb + 1), :], in_=windows[nb][:])
        elif TAIL_G:
            e = E - 1
            tail_pass(0)
            tail_pass(1)
            for nb in range(2):
                y_nb = hid.tile([P, C], F32, name="y")
                nc.scalar.copy(out=y_nb[:], in_=tail_sums[nb][:])
                nc.vector.tensor_tensor(
                    out=windows[nb][:].indirect(offsets[:, C * e // 16 : C * (e + 1) // 16]),
                    in0=y_nb[:],
                    in1=gate_of(e, nb, 0, 2),
                    op=MULT,
                )
                nc.sync.dma_start(out=out[P * nb : P * (nb + 1), :], in_=windows[nb][:])
        elif TAIL_NB:
            e = E - 1
            tail_codes, tail_scales = {}, {}
            for s in range(2):
                tail_codes[s] = hid.tile([P, 2, HALF], U32, name="hcodes", align_bytes=64)
                tail_scales[s] = hid.tile([P, 2, HALF], U8, name="hscales", align_bytes=64)
                nc.vector.quantize_mx(
                    out=tail_codes[s][:].rearrange("p g n -> p (g n)").bitcast(FP8X4),
                    scales=tail_scales[s][:].rearrange("p g n -> p (g n)"),
                    in_=hidden[e][:, s, :, :, :].rearrange("p g n t -> p (g n t)"),
                )
            c2, s2 = q_w2[e]
            for nb in range(2):
                py = psum_y.tile([P, 2, HALF], F32, name="py")
                for s in range(2):
                    for g in range(2):
                        nc.tensor.matmul_mx(
                            out=py[:, s, :],
                            lhsT=c2[:, g, P * nb : P * (nb + 1)].bitcast(FP8X4),
                            lhsT_scale=s2[:, g, P * nb : P * (nb + 1)],
                            rhs=tail_codes[s][:, g, :].bitcast(FP8X4),
                            rhs_scale=tail_scales[s][:, g, :],
                            start=(g == 0),
                            stop=(g == 1),
                        )
                y_nb = hid.tile([P, C], F32, name="y")
                nc.scalar.copy(out=y_nb[:], in_=py[:].rearrange("p s n -> p (s n)"))
                nc.vector.tensor_tensor(
                    out=windows[nb][:].indirect(offsets[:, C * e // 16 : C * (e + 1) // 16]),
                    in0=y_nb[:],
                    in1=gate_of(e, nb, 0, 2),
                    op=MULT,
                )
                nc.sync.dma_start(out=out[P * nb : P * (nb + 1), :], in_=windows[nb][:])
        else:
            for s in range(2):
                second_layer(E - 1, s, s + 1)
            for s in range(2):
                copy_y(E - 1, s, s + 1)
            for s in range(2):
                for nb in range(2):
                    scatter(E - 1, s, s + 1, nb)

            for nb in range(2):
                nc.sync.dma_start(out=out[P * nb : P * (nb + 1), :], in_=windows[nb][:])
